import numpy as np, ml_dtypes
CORES = [9,25,41,57]
N = 4
import mx_ref
BF = ml_dtypes.bfloat16
def gentries(a):
    return np.ascontiguousarray(a.reshape(8, 16, -1).transpose(0, 2, 1)).reshape(8, -1)
def gtable(e):
    e = np.asarray(e); return np.ascontiguousarray(e.reshape(8, -1, 16).transpose(0, 2, 1)).reshape(128, -1).astype(np.int32)
def gpick(z, e):
    return np.concatenate([z[16 * g:16 * g + 16][:, e[g]] for g in range(8)])
def cols(t, e):
    v = np.concatenate([t.reshape(128, -1, 4), np.zeros((128, 1, 4), BF)], axis=1)
    return np.ascontiguousarray(v[:, e]).reshape(128, -1)
def pick(q, e):
    c = np.concatenate([q[0].reshape(128, -1, 4), np.zeros((128, 1, 4), np.uint8)], axis=1); s = np.concatenate([q[1], np.ones((16, 1), np.uint8)], axis=1)
    return (np.ascontiguousarray(c[:, e].reshape(128, -1)), np.ascontiguousarray(s[:, e]))
def join(*qs):
    return (np.concatenate([q[0] for q in qs], axis=1), np.concatenate([q[1] for q in qs], axis=1))
def put(q, e, v):
    c, s = q[0].reshape(128, -1, 4).copy(), q[1].copy(); c[:, e] = v[0].reshape(128, -1, 4); s[:, e] = v[1]
    return (c.reshape(128, -1), s)
def pk(c, s):
    return (np.ascontiguousarray(c), mx_ref.live(s))
def emit(q):
    return q[0], q[1]
def values_of_codes():
    e, c = np.zeros((128, 128, 4), np.float32), np.zeros((128, 2, 4), np.uint8)
    e[np.arange(128), np.arange(128), 0] = 1
    c[:127, :, 0] = np.arange(256).reshape(2, 128).T[:127]
    return mx_ref.matmul(mx_ref.quantize(e.reshape(128, 512).astype(BF)), (c.reshape(128, 8), np.full((16, 2), 127, np.uint8))).T.reshape(-1).astype(np.float64)
CODE_VALUE, SCALE_VALUE = values_of_codes(), 2.0 ** (np.arange(256) - 127.0)
def decode(q):
    return (CODE_VALUE[q[0]].reshape(16, 8, -1, 4) * SCALE_VALUE[q[1]][:, None, :, None] + 0.0).reshape(128, -1).astype(np.float32)
def f(rng, *shape):
    return mx_ref.flush((rng.standard_normal(shape, dtype=np.float32) * np.exp2(rng.integers(-2, 3, shape[:-1] + (1,)))).astype(BF))
def wide(rng, *shape, cols=0):
    v = rng.standard_normal(shape, dtype=np.float32) * np.exp2(rng.integers(-12, 13, shape)).astype(np.float32)
    if cols: v *= np.repeat(np.exp2(rng.integers(-cols, cols + 1, shape[:-2] + (1, shape[-1] // 4))) * (rng.random(shape[:-2] + (1, shape[-1] // 4)) > 0.0625), 4, axis=-1).astype(np.float32)
    return mx_ref.flush(v.astype(BF))
T, S, CAPP, R = 3, 384, 16, 2
def coarse(v):
    v = v.astype(np.float32)
    v[np.abs(v) < np.float32(2.0 ** -16)] = 0
    return v.astype(BF)
def numbers_of(rng):
    return {"x": coarse(f(rng, N, 128, 512 * T)), "e": coarse(f(rng, N, 128, 4 * S)), "v": np.array(f(rng, N, 128, 512))}
def lists_of(rng):
    return {k: np.stack([gtable(rng.integers(0, S, (8, S))) for r in range(N)]) for k in ("pa", "pb")}
def signs(rng):
    return np.stack([rng.permutation(128) % 2 * 2.0 - 1.0 for r in range(N)]).astype(np.float32)
def setup_inputs(rng):
    return {**numbers_of(rng), **lists_of(rng)}
def setup_inputs_ties(rng):
    d = setup_inputs(rng)
    x = d["x"].reshape(N, 128, T, 128, 4)
    x[:, :, :, ::8] = 0
    for r in range(N):
        run = np.concatenate([rng.permutation(4), rng.permutation(4)])
        k = run[np.arange(S) * 8 // S]
        d["e"][r] = cols(d["e"][r], np.where(k == 3, -1, k))
        same = np.argsort(k, kind="stable").reshape(4, S // 4)
        a, b = gentries(d["pa"][r]), gentries(d["pb"][r])
        d["pb"][r] = gtable(np.where(rng.random((8, S)) < 0.5, same[k[a], rng.integers(0, S // 4, (8, S))], b))
    return {**d, "x": x.reshape(N, 128, 512 * T)}
def setup_inputs_near(rng):
    d = setup_inputs(rng)
    x = d["x"].reshape(N, 128, T, 128, 4)
    x[:, :96] = 0
    x[:, 0, :, :, 0] = signs(rng)[:, None, :].astype(BF)
    x[:, 8:10] = (rng.choice([-1.0, 1.0], (N, 2, T, 128, 4)) * 2.0 ** -4).astype(np.float32).astype(BF)
    e = d["e"].reshape(N, 128, S, 4)
    m = np.zeros((N, 128), bool)
    for r in range(N): m[r, 32 + 8 * r:40 + 8 * r] = True
    e[~m] = 0
    e[:, 0, :, 0] = 1
    s = np.arange(S) // 2
    g = (((s[:, None] >> np.arange(8)) & 1) * np.exp2(np.arange(8) - 19.0)).astype(np.float32).astype(BF)
    e[:, 8] = g[:, :4]
    e[:, 9] = g[:, 4:]
    for r in range(N):
        d["pb"][r] = gtable(gentries(d["pa"][r]) ^ rng.choice(np.array([1, 2, 2, 4]), (8, S)))
    small = np.float32(2.0 ** -8)
    return {**d, "x": (x.astype(np.float32) * small).astype(BF).reshape(N, 128, 512 * T), "e": (e.astype(np.float32) * small).astype(BF).reshape(N, 128, 4 * S)}
def setup_inputs_huge(rng):
    d = setup_inputs(rng)
    g = (rng.permutation(N) % 2 * 2.0 - 1.0) * 2.0 ** 26
    x = rng.integers(12, 16, (N, 128, T, 128, 4)) * 2.0 ** 26 * signs(rng)[:, None, None, :, None]
    e = rng.permuted(np.tile(np.arange(512) % 4 + 12, (N, S, 1)), axis=2).reshape(N, S, 128, 4).transpose(0, 2, 1, 3) * g[:, None, None, None]
    d["x"] = x.astype(np.float32).reshape(N, 128, 512 * T).astype(BF)
    d["e"] = np.ascontiguousarray(e.astype(np.float32)).reshape(N, 128, 4 * S).astype(BF)
    return d
def setup_inputs_crowd(rng):
    d = setup_inputs(rng)
    x = d["x"].reshape(N, 128, T, 128, 4)
    e = d["e"].reshape(N, 128, S, 4)
    x[:, 0:8 * N:8] = 0
    e[:, 0:8 * N:8] = 0
    e[:, np.arange(S) // (S // N) * 8, np.arange(S), 0] = 1024
    o = rng.permutation(N)
    rest = np.array([c for c in o if c not in (o[0], o[1], o[3])])
    for r in range(N):
        to = np.full(128, o[1])
        if r != o[0] and r != o[1]:
            to[:CAPP] = o[0]
            to[2 * CAPP + 1:] = np.resize(rest, 128 - 2 * CAPP - 1)
        to = rng.permutation(to)
        x[r, 8 * to, T - 1, np.arange(128), 0] = 4096
    return {**d, "x": x.reshape(N, 128, 512 * T), "e": e.reshape(N, 128, 4 * S)}
def setup_inputs_spread(rng):
    d = setup_inputs(rng)
    d["x"] = coarse(wide(rng, N, 128, 512 * T, cols=6))
    d["e"] = coarse(wide(rng, N, 128, 4 * S))
    return d
def check_inputs(d):
    b = []
    for k in ("x", "e", "v"):
        a = np.abs(d[k].astype(np.float32))
        if not (np.isfinite(a).all() and ((a == 0) | (a >= 2.0 ** -30) & (a <= 2.0 ** 30)).all()): b.append("a value of " + k)
    for k in ("pa", "pb"):
        if not ((d[k] >= 0) & (d[k] < S)).all(): b.append("an entry of " + k)
    return b
def trace(q, w, a, b):
    p = np.arange(128)
    s = mx_ref.matmul(pick(q, p), w)
    came = []
    for t in range(1, T):
        m, n = gpick(s, a), gpick(s, b)
        came.append(np.where(n > m, np.repeat(b, 16, axis=0), np.repeat(a, 16, axis=0)))
        s = np.maximum(m, n) + mx_ref.matmul(pick(q, 128 * t + p), w)
    path = np.zeros((128, T), int)
    path[:, T - 1] = np.argmax(s + np.float32(0.0), axis=1)
    for t in range(T - 1, 0, -1): path[:, t - 1] = came[t - 1][p, path[:, t]]
    return path
def reference(x, e, v, pa, pb):
    a, b = [gentries(pa[r]) for r in range(N)], [gentries(pb[r]) for r in range(N)]
    qe = [mx_ref.quantize(e[r]) for r in range(N)]
    data = join(*[mx_ref.quantize(x[r]) for r in range(N)])
    mine = [128 * T * r + np.arange(128 * T) for r in range(N)]
    for turn in range(R):
        home = [trace(pick(data, mine[r]), qe[r], a[r], b[r]) for r in range(N)]
        visit, at, new = [], [], []
        for c in range(N):
            slot = np.full((T, 128), -1)
            for r in range(N):
                p = np.flatnonzero(home[r][:, T - 1] // (S // N) == c)[:CAPP]
                slot[:, CAPP * r:CAPP * r + len(p)] = 128 * T * r + 128 * np.arange(T)[:, None] + p
            slot = slot.reshape(-1)
            q = pick(data, slot)
            path = trace(q, qe[c], a[c], b[c])
            z = (decode(q) + decode(pick(qe[c], path.transpose().reshape(-1)))) * np.float32(0.5)
            full = np.flatnonzero(slot >= 0)
            at.append(slot[full])
            new.append(pick(mx_ref.quantize(np.ascontiguousarray(z.astype(BF))), full))
            visit.append(path)
        data = put(data, np.concatenate(at), join(*new))
    y, ol, dl = np.zeros((N, 128, 128 * T), np.float32), np.zeros((N, 128, T), np.float32), np.zeros((N, N * CAPP, T), np.float32)
    oc, osc = np.zeros((N, 128, 512 * T), np.uint8), np.zeros((N, 16, 128 * T), np.uint8)
    for r in range(N):
        q = pick(data, mine[r])
        y[r] = mx_ref.matmul(mx_ref.quantize(v[r]), q)
        ol[r] = home[r]
        dl[r] = visit[r][:N * CAPP]
        oc[r], osc[r] = emit(q)
    return {"y": y, "ol": ol, "dl": dl, "oc": oc, "osc": osc}

@@ -1,0 +1,485 @@
+from concourse.bass import DstId, RemoteDMATransfer
+from concourse.mybir import dt, AluOpType, ActivationFunctionType
+
+N = 4
+NT = 3
+NS = 384
+CAP = 16
+RUN = CAP * NT
+ST = 144
+OLD = ST * NT
+LOW = -9.0e29
+UW = 520
+
+C4 = "float8_e4m3fn_x4"
+SCRATCH = {}
+
+
+def _pair(name, n):
+    SCRATCH[name + "c"] = ("sbuf", [128, n], C4)
+    SCRATCH[name + "s"] = ("sbuf", [128, n], "uint8")
+
+
+for _n, _w in (("d1", OLD), ("d2", OLD), ("d3", 128 * NT), ("m1", OLD + N * RUN), ("m2", OLD + N * RUN),
+               ("qe", NS), ("qv", 128), ("qu", 512), ("s1", 3 * RUN), ("s2", 3 * RUN), ("l1", N * RUN),
+               ("l2", N * RUN), ("x1", 128 * NT), ("x2", 128 * NT), ("n1", N * RUN), ("n2", N * RUN)):
+    _pair(_n, _w)
+for _n, _w in (("xt", 4 * OLD), ("et", 4 * NS), ("vt", 512), ("ut", 2 * UW), ("bt1", 4 * N * RUN), ("bt2", 4 * N * RUN)):
+    SCRATCH[_n] = ("sbuf", [128, _w], "bfloat16")
+for _n, _w in (("a0", NS), ("a1", NS), ("f2", NS), ("uu", NS), ("ww", NS), ("rr", NS), ("jk", NS), ("wh", 6 * NS),
+               ("wv", 6 * NS), ("de", 4 * NS), ("dc", 2 * N * RUN), ("ge", 2 * N * RUN), ("jj", 2 * NS),
+               ("j16", 128), ("msk", 128), ("rs", 128), ("cd", 128), ("bb", 128), ("tr", 128), ("oh", 128),
+               ("cum", 128), ("j2", 128), ("jid", 128), ("pm", 4), ("c13", 16), ("cx", 24), ("con", 4), ("c1", 4),
+               ("c2", 4), ("z4", 4), ("cj0", 4), ("cj", 4), ("val", 64), ("ct0", 24), ("ct", 24), ("one", 8),
+               ("gg", 64), ("gs2", 64), ("gs1", 64), ("nf", 16), ("row1", 192), ("row2", 192), ("mk", 128),
+               ("rho", 128), ("mx", 24), ("dfv", 24), ("dfh", 24), ("po", 4), ("pd", 12), ("ys", 128 * NT)):
+    SCRATCH[_n] = ("sbuf", [128, _w], "float32")
+for _n, _w in (("pi", 4), ("ph", 48), ("pv", 48)):
+    SCRATCH[_n] = ("sbuf", [128, _w], "int32")
+for _n, _w in (("lh", 72), ("lv", 72), ("fl1", 16), ("fl2", 16), ("xl", 24), ("onl", 4), ("zl", 2), ("o2", 4),
+               ("o1", 4), ("bl1", 12), ("bl2", 12), ("so", 4), ("ml1", 24), ("ml2", 24)):
+    SCRATCH[_n] = ("sbuf", [128, _w], "uint16")
+PSUM = ("pa0", "pb0", "pf1", "pf2", "pd0", "pd1", "pd2", "pd3")
+for _n in PSUM:
+    SCRATCH[_n] = ("psum", [128, 512], "float32")
+
+SEMAPHORES = (["cv", "cs", "cp", "cg", "dx0", "deh", "dx1", "dx2", "ddup", "dv", "del", "dp", "loc", "out1", "out2"]
+              + ["ac%d" % k for k in range(4)] + ["as%d" % k for k in range(4)])
+
+ADD, SUB, MUL, MAX = AluOpType.add, AluOpType.subtract, AluOpType.mult, AluOpType.max
+EQ, GT, GE = AluOpType.is_equal, AluOpType.is_gt, AluOpType.is_ge
+COPY, SIGN = ActivationFunctionType.Copy, ActivationFunctionType.Sign
+
+
+def _meet(a, b):
+    if a[2] <= b[1] or b[2] <= a[1] or a[4] <= b[3] or b[4] <= a[3]:
+        return False
+    if a[5] == 1 and b[5] == 1:
+        return True
+    return len(set(range(a[3], a[4], a[5])) & set(range(b[3], b[4], b[5]))) > 0
+
+
+def rank_program(g, core, T, topo):
+    r = T.rank_of(core)
+    if r is None:
+        return
+    eng = {"v": g.vector, "s": g.scalar, "p": g.tensor, "g": g, "y": g.sync}
+    own = {"v": "cv", "s": "cs", "p": "cp", "g": "cg"}
+    count = {}
+    known = {q: {} for q in eng}
+    hist = {}
+
+    def W(name, c0=0, c1=None, st=1, p0=0, p1=128):
+        if c1 is None:
+            c1 = SCRATCH[name][1][1]
+        ap = T[name][p0:p1, c0:c1] if st == 1 else T[name][p0:p1, c0:c1:st]
+        if name in PSUM:
+            return (ap, [(name, 0, 128, 0, 512, 1)])
+        return (ap, [(name, p0, p1, c0, c1, st)])
+
+    def by(win, off):
+        return (win[0].indirect(off[0]), win[1] + off[1])
+
+    def wait(q, tok):
+        sem, val, clock = tok
+        if known[q].get(sem, 0) >= val:
+            return
+        eng[q].wait_ge(T.sem[sem], val)
+        known[q][sem] = val
+        for k in clock:
+            if known[q].get(k, 0) < clock[k]:
+                known[q][k] = clock[k]
+
+    def order(q, reads, writes):
+        need = {}
+        for some, wr in ((reads, False), (writes, True)):
+            for reg in some:
+                for (oreg, owr, oq, tok) in hist.get(reg[0], []):
+                    clash = wr or owr or (reg[0] in PSUM and oq != q)
+                    if clash and _meet(reg, oreg) and (tok[0] not in need or need[tok[0]][1] < tok[1]):
+                        need[tok[0]] = tok
+        for k in sorted(need, key=lambda s: s == own.get(q)):
+            wait(q, need[k])
+
+    def note(q, reads, writes, tok):
+        for reg in reads:
+            hist.setdefault(reg[0], []).append((reg, False, q, tok))
+        for reg in writes:
+            hist.setdefault(reg[0], []).append((reg, True, q, tok))
+
+    def regs(views):
+        out = []
+        for v in views:
+            if isinstance(v, tuple):
+                out = out + v[1]
+        return out
+
+    def op(q, make, ins, outs):
+        reads, writes = regs(ins), regs(outs)
+        order(q, reads, writes)
+        sem = own[q]
+        count[sem] = count.get(sem, 0) + 1
+        make().then_inc(T.sem[sem], 1)
+        note(q, reads, writes, (sem, count[sem], dict(known[q])))
+
+    def dma(q, out, in_, sem, total=1):
+        reads, writes = regs([in_]), regs([out])
+        order(q, reads, writes)
+        count[sem] = count.get(sem, 0) + 16
+        eng[q].dma_start(out[0], in_[0]).then_inc(T.sem[sem], 16)
+        note(q, reads, writes, (sem, 16 * total, dict(known[q])))
+
+    def hbm(ap):
+        return (ap, [])
+
+    def val_of(s):
+        return s[0] if isinstance(s, tuple) else s
+
+    def copy(q, out, in_):
+        if q == "v":
+            op("v", lambda: g.vector.tensor_copy(out[0], in_[0]), [in_], [out])
+        else:
+            op("s", lambda: g.scalar.activation(out[0], in_[0], COPY), [in_], [out])
+
+    def tt(out, a, b, o):
+        op("v", lambda: g.vector.tensor_tensor(out[0], a[0], b[0], o), [a, b], [out])
+
+    def ts(out, a, s1, o1, s2=None, o2=None):
+        if o2 is None:
+            op("v", lambda: g.vector.tensor_scalar(out[0], a[0], val_of(s1), None, o1), [a, s1], [out])
+        else:
+            op("v", lambda: g.vector.tensor_scalar(out[0], a[0], val_of(s1), val_of(s2), o1, o2), [a, s1, s2], [out])
+
+    def scan(out, a, b, init, o1, o2):
+        op("v", lambda: g.vector.tensor_tensor_scan(out[0], a[0], b[0], init, o1, o2), [a, b], [out])
+
+    def fill(out, c):
+        op("v", lambda: g.vector.memset(out[0], c), [], [out])
+
+    def signs(acc, junk, in_, bias):
+        op("s", lambda: g.scalar.activation(junk[0], in_[0], SIGN, bias=bias[0], scale=-1.0, accum_out=acc[0]),
+           [in_, bias], [junk, acc])
+
+    def iota(out, pattern, base, ch=0, whole=False):
+        if whole:
+            op("g", lambda: g.iota(out[0], pattern, base, ch), [], [out])
+        else:
+            op("g", lambda: g.iota(out[0], pattern, base, ch, allow_small_or_imprecise_dtypes=True), [], [out])
+
+    def quant_at(name, c0, n, tile, at):
+        c, s, t = W(name + "c", c0, c0 + n), W(name + "s", c0, c0 + n), W(tile, at, at + 4 * n)
+        op("v", lambda: g.vector.quantize_mx(c[0], s[0], t[0]), [t], [c, s])
+
+    def quant(name, c0, n, tile, e0):
+        quant_at(name, c0, n, tile, 4 * e0)
+
+    def mm(bank, a, a0, b, b0, n):
+        o = W(bank, 0, n)
+        ac, as_, bc, bs = W(a + "c", a0, a0 + 128), W(a + "s", a0, a0 + 128), W(b + "c", b0, b0 + n), W(b + "s", b0, b0 + n)
+        op("p", lambda: g.tensor.matmul_mx(o[0], ac[0], as_[0], bc[0], bs[0], True, True), [ac, as_, bc, bs], [o])
+
+    def pickc(dst, c0, src, off, o0, k):
+        o, w, f = W(dst + "c", c0, c0 + 16 * k), W(src + "c"), W(off, o0, o0 + k)
+        op("v", lambda: g.vector.tensor_copy(o[0].bitcast(dt.uint32), w[0].bitcast(dt.uint32).indirect(f[0])), [w, f], [o])
+
+    def picks(dst, c0, src, off, o0, k):
+        copy("s", W(dst + "s", c0, c0 + 16 * k), by(W(src + "s"), W(off, o0, o0 + k)))
+
+    def pick(dst, c0, src, off, o0, k):
+        pickc(dst, c0, src, off, o0, k)
+        picks(dst, c0, src, off, o0, k)
+
+    dests = [(r + 1 + k) % N for k in range(N)]
+
+    def engines_of(a, b, k, part):
+        e = topo.engines(T.cores[a], T.cores[b])
+        h, f = len(e) // 2, len(e) // 4
+        return ((e[:h], e[h:h + f], e[h + f:]), (e[h:], e[:f], e[f:h]))[part][k]
+
+    def send(phase, src, at, dst, base):
+        for part, tag, sem in ((0, "c", "ac%d" % phase), (1, "s", "as%d" % phase)):
+            moves, reads = [], []
+            for k in range(N - 1):
+                d = dests[k]
+                rid, pid, _ = topo.addr(T.cores[d])
+                a = W(src + tag, at(k), at(k) + RUN)
+                b = W(dst + tag, base + RUN * r, base + RUN * (r + 1))
+                reads = reads + a[1]
+                m = sum(1 << e for e in engines_of(r, d, k, part))
+                moves.append(RemoteDMATransfer(
+                    dst_ids=[DstId(rid=rid, pnc=pid)], dma_engine_mask=m, remote_sem=T.sem[sem],
+                    src=a[0].bitcast(dt.uint8) if part == 0 else a[0], dst=b[0].bitcast(dt.uint8) if part == 0 else b[0]))
+                count["loc"] = count.get("loc", 0) + len(engines_of(r, d, k, part))
+            order("g", reads, [])
+            g.remote_dma_fused(moves, local_sem=T.sem.loc)
+            total = sum(len(engines_of((r - 1 - k) % N, r, k, part)) for k in range(N - 1))
+            count[sem] = total
+            for h in range(N):
+                if h != r:
+                    note("far", [], W(dst + tag, base + RUN * h, base + RUN * (h + 1))[1], (sem, total, {}))
+
+    PM, PF, IB = W("pm", 0, 1), W("pm", 1, 2), W("pm", 2, 3)
+    H, G = NS // 2, 256
+    C = N * RUN
+
+    dma("y", W("xt", 0, 512), hbm(T.x[:, 0:512]), "dx0")
+    dma("s", W("et", 0, 4 * G), hbm(T.e[:, 0:4 * G]), "del")
+    dma("y", W("et", 4 * G, 4 * NS), hbm(T.e[:, 4 * G:4 * NS]), "deh")
+    dma("s", W("ph", 0, 24), hbm(T.pa[:, :]), "dp", 2)
+    dma("s", W("ph", 24, 48), hbm(T.pb[:, :]), "dp", 2)
+    for t in (1, 2):
+        dma("y", W("xt", 4 * ST * t, 4 * ST * t + 512), hbm(T.x[:, 512 * t:512 * t + 512]), "dx%d" % t)
+    for h in range(N):
+        for u in range(2):
+            p0 = 32 * h + 16 * u
+            dma("y", W("pv", 0, 24, 1, p0, p0 + 16), hbm(T.pa[16 * h:16 * h + 16, :]), "ddup", 4 * N)
+            dma("y", W("pv", 24, 48, 1, p0, p0 + 16), hbm(T.pb[16 * h:16 * h + 16, :]), "ddup", 4 * N)
+    dma("y", W("vt"), hbm(T.v[:, :]), "dv")
+
+    iota(W("pi", 0, 1), [[0, 1]], 0, 1, True)
+    iota(W("jid"), [[1, 128]], 0)
+    iota(W("c13", 0, 9), [[0, 3], [2 * ST, 3]], 128)
+    iota(W("c13", 9, 14), [[2 * ST, 5]], 128 - 2 * ST)
+    iota(W("cx"), [[16, NT], [RUN, N], [0, 2]], 0)
+    iota(W("j16"), [[0, 8], [1, 16]], 0)
+    iota(W("con", 0, 3), [[16, 3]], RUN * r)
+    iota(W("c1"), [[NS, 4]], 0)
+    iota(W("c2"), [[-2 * NS, 2], [NS, 2]], 4 * NS)
+    iota(W("cj0"), [[16, 4]], 0)
+    iota(W("ct0"), [[128, NT], [16, 8]], 0)
+    iota(W("jj"), [[1, 2 * NS]], -NS)
+    fill(W("ut"), 0.0)
+    for t in range(NT):
+        fill(W("xt", 4 * (ST * t + 128), 4 * (ST * t + 130)), 0.0)
+    copy("v", PF, W("pi", 0, 1))
+    ts(W("pi", 1, 2), W("pi", 0, 1), 15, AluOpType.bitwise_and)
+    fill(W("z4"), 0.0)
+    fill(W("zl"), 128)
+    for u in range(2):
+        ts(W("ut", UW * u + 2 + u, UW * u + 514, 4), W("jid"), PF, EQ, 0.5, MUL)
+    copy("v", PM, W("pi", 1, 2))
+    for k in range(N):
+        fill(W("cd", 32 * k, 32 * k + 32), float(dests[k]))
+    ts(IB, PM, 0.5, ADD)
+    for b in range(4):
+        quant_at("qu", 128 * b, 128, "ut", UW * (b % 2) + (2 if b < 2 else 0))
+
+    def decode(x, stride, lst, w, prep, extra=None, tail=None, late=False):
+        cut = G if late else 224
+        prep(0)
+        mm("pa0", x, 0, "qe", 0, cut)
+        mm("pb0", x, 0, "qe", cut, NS - cut)
+        if not late:
+            prep(1)
+            mm("pf1", x, stride, "qe", 0, NS)
+            prep(2)
+            mm("pf2", x, 2 * stride, "qe", 0, NS)
+        copy("v" if late else "s", W("a0", 0, cut), W("pa0", 0, cut))
+        copy("s" if late else "v", W("a0", cut, NS), W("pb0", 0, NS - cut))
+        copy("s", W(w, 128, NS), by(W("a0"), W(lst, 8, 24)))
+        copy("v", W(w, 0, 128), by(W("a0"), W(lst, 0, 8)))
+        if late:
+            prep(1)
+            mm("pf1", x, stride, "qe", 0, NS)
+        tt(W(w, NS, NS + 128), by(W("a0"), W(lst, 24, 32)), W(w, 0, 128), MAX)
+        if late:
+            prep(2)
+            mm("pf2", x, 2 * stride, "qe", 0, NS)
+        tt(W(w, NS + 128, 2 * NS), by(W("a0"), W(lst, 32, 48)), W(w, 128, NS), MAX)
+        tt(W("a1", 0, 128), W(w, NS, NS + 128), W("pf1", 0, 128), ADD)
+        tt(W("a1", 128, NS), W(w, NS + 128, 2 * NS), W("pf1", 128, NS), ADD)
+        copy("s", W("f2"), W("pf2", 0, NS))
+        if extra is not None:
+            extra()
+        copy("s", W(w, 4 * NS, 4 * NS + H), by(W("a1"), W(lst, 0, 12)))
+        copy("s", W(w, 4 * NS + H, 5 * NS), by(W("a1"), W(lst, 12, 24)))
+        if tail is None:
+            copy("s", W(w, 5 * NS, 6 * NS), by(W("a1"), W(lst, 24, 48)))
+        else:
+            tail()
+        tt(W("ww"), by(W("a1"), W(lst, 24, 48)), W("f2"), ADD)
+        tt(W("uu", 0, H), W(w, 4 * NS, 4 * NS + H), W("pf2", 0, H), ADD)
+        tt(W("uu", H, NS), W(w, 4 * NS + H, 5 * NS), W("pf2", H, NS), ADD)
+        scan(W("rr"), W("uu"), W("ww"), LOW, MAX, MAX)
+
+    def spread(name, blocks):
+        for a in range(4):
+            b = a ^ 1
+            copy("v", W(name, blocks[a][0], blocks[a][1], 1, 32 * b, 32 * b + 32),
+                 W(name, blocks[a][0], blocks[a][1], 1, 32 * a, 32 * a + 32))
+        copy("v", W(name, blocks[0][0], blocks[1][1], 1, 64, 128), W(name, blocks[0][0], blocks[1][1], 1, 0, 64))
+        copy("v", W(name, blocks[2][0], blocks[3][1], 1, 0, 64), W(name, blocks[2][0], blocks[3][1], 1, 64, 128))
+
+    def admit(fl):
+        top = W("rr", NS - 1, NS)
+        signs(W("one", 0, 1), W("j2", 0, 3), W("rr", NS // N - 1, NS - 1, NS // N), top)
+        ts(W("bb"), W("cd"), W("one", 0, 1), EQ)
+        op("v", lambda: g.vector.transpose(W("tr")[0], W("bb")[0]), [W("bb")], [W("tr")])
+        for a in range(4):
+            for k in range(4):
+                copy("v" if (a + k) % 2 == 0 else "s", W("oh", 32 * a, 32 * a + 32, 1, 32 * k, 32 * k + 32),
+                     W("tr", 32 * k, 32 * k + 32, 1, 32 * a, 32 * a + 32))
+        scan(W("cum"), W("oh"), W("oh"), 0.0, ADD, MAX)
+        signs(W("one", 1, 2), W("j2"), W("cum"), IB)
+        ts(W(fl, 0, 14), W("c13", 0, 14), W("one", 1, 2), ADD, 0.5, MUL)
+        spread(fl, ((0, 3), (3, 6), (6, 9), (10, 13)))
+
+    def back(w, put, meanwhile):
+        s2 = W("one", 2, 3)
+        signs(s2, W("jk"), W("rr"), W("rr", NS - 1, NS))
+        meanwhile()
+        ts(W("o2"), W("c2"), s2, ADD)
+        for t, off, gs in ((2, "o2", "gs2"), (1, "o1", "gs1")):
+            tt(W("gg"), by(W(w), W(off)), W("msk", 0, 64), MUL)
+            if t == 2:
+                put(2, s2, 0.0)
+            else:
+                put(1, W("gs2", 47, 48), W("one", 5, 6))
+            scan(W(gs), W("rs", 0, 64), W("gg"), 0.0, MUL, ADD)
+            dd = W("one", 3 + t, 4 + t)
+            ts(dd, W(gs, 31, 32), W(gs, 15, 16), GT, W(gs, 63, 64), MUL)
+            if t == 2:
+                ts(W("o1"), W("c1"), W(gs, 47, 48), ADD, dd, ADD)
+        put(0, W("gs1", 47, 48), W("one", 4, 5))
+
+    def merge_list(fl, row, ml, between):
+        def gap():
+            if between:
+                between.pop(0)()
+        ts(W("nf", 4, 7), W(fl, 0, 9, 3), -127.0, ADD, 0.0, MAX)
+        ts(W("nf", 7, 8), W(fl, 10, 11), -127.0, ADD, 0.0, MAX)
+        copy("v", W("nf", 0, 3), W(fl, 0, 9, 3))
+        copy("v", W("nf", 3, 4), W(fl, 10, 11))
+        tt(W("nf", 8, 12), W("nf", 4, 8), W("cj"), MUL)
+        gap()
+        tt(W("nf", 12, 16), W("nf", 8, 12), W("nf", 0, 4), ADD)
+        gap()
+        copy("v", W("so"), W("nf", 12, 16))
+        gap()
+        win = W(row)
+        op("v", lambda: g.vector.tensor_copy(win[0].indirect(W("so")[0]), W("val")[0]), [W("so"), W("val")], [win])
+        gap()
+        tt(W("mk"), W(row, 0, 128), W("msk"), MUL)
+        gap()
+        scan(W("rho"), W("rs"), W("mk"), 0.0, MUL, ADD)
+        gap()
+        for t in range(NT):
+            tt(W("mx", 8 * t, 8 * t + 8), W("rho", 15, 128, 16), W("ct", 8 * t, 8 * t + 8), MAX)
+        for t in range(NT):
+            ts(W(ml, 8 * t, 8 * t + 8), W("mx", 8 * t, 8 * t + 8), float(16 * t), ADD)
+        while between:
+            gap()
+
+    def table_a(lst, w):
+        copy("s", W(w, 2 * NS, 3 * NS), by(W("jj", NS, 2 * NS), W(lst, 0, 24)))
+
+    def table_d(lst, w):
+        copy("s", W(w, 3 * NS, 4 * NS), by(W("jj"), W(lst, 48, 72)))
+
+    def first(t):
+        if t == 0:
+            quant("d1", 0, 130, "xt", 0)
+            quant("qe", 0, G, "et", 0)
+            quant("qe", G, NS - G, "et", G)
+            copy("v", W("lh", 0, 48), W("ph"))
+        else:
+            quant("d1", ST * t, 130, "xt", ST * t)
+
+    def unpack_e():
+        for b in range(4):
+            mm("pd%d" % b, "qu", 128 * b, "qe", 0, NS)
+        for b in range(2):
+            copy("s", W("de", NS * b, NS * b + NS), W("pd%d" % b, 0, NS))
+
+    for turn in (1, 2):
+        d, s, l, x, n, m = ("%s%d" % (c, turn) for c in "dslxnm")
+        fl, bl, bt, ml, row = ("%s%d" % (c, turn) for c in ("fl", "bl", "bt", "ml", "row"))
+        if turn == 1:
+            decode(d, ST, "lh", "wh", first, None, unpack_e, True)
+        else:
+            decode(d, ST, "lh", "wh", lambda t: pick("d2", ST * t, "m1", "ml1", 8 * t, 8))
+        admit(fl)
+        pick(s, 0, d, fl, 0, 9)
+        send(2 * turn - 2, s, lambda k: RUN * k, l, 0)
+        pick(l, RUN * r, d, fl, 10, 3)
+        if turn == 1:
+            copy("v", W("lv", 0, 48), W("pv"))
+            tt(W("dfv"), W("pv", 24, 48), W("pv", 0, 24), SUB)
+            ts(W("xl"), W("cx"), PM, ADD)
+            ts(W("msk"), W("j16"), PM, EQ)
+            ts(W("lv", 48, 72), W("dfv"), float(NS), ADD)
+            table_a("lv", "wv")
+            table_d("lv", "wv")
+            for b in (2, 3):
+                copy("v", W("de", NS * b, NS * b + NS), W("pd%d" % b, 0, NS))
+            ts(W("rs"), W("j16"), 1.0, GE)
+            ts(W("onl", 0, 3), W("con", 0, 3), PM, ADD)
+            ts(W("cj"), W("cj0"), PM, ADD)
+            ts(W("ct"), W("ct0"), PM, ADD)
+            for k in range(N):
+                ts(W("val", 16 * k, 16 * k + 16), W("j16", 0, 16), float(OLD + RUN * dests[k]), ADD)
+            fill(W("row1"), 0.0)
+        else:
+            def old_codes():
+                for t in range(2):
+                    pickc("m2", ST * t, "m1", "ml1", 8 * t, 8)
+            back("wh", lambda t, a, b: ts(W("po", t, t + 1), W("z4", 0, 1), a, ADD, b, ADD), old_codes)
+            dma("y", hbm(T.ol[:, :]), W("po", 0, 3), "out1")
+            for t in range(NT):
+                picks("m2", ST * t, "m1", "ml1", 8 * t, 8)
+
+        def halves():
+            for b in range(4):
+                mm("pd%d" % b, "qu", 128 * b, l, 0, C)
+            for b in range(2):
+                copy("s", W("dc", C * b, C * (b + 1)), W("pd%d" % b, 0, C))
+
+        def idle():
+            if turn == 1:
+                for t in range(NT):
+                    quant("m1", ST * t, 130, "xt", ST * t)
+            else:
+                pickc("m2", ST * 2, "m1", "ml1", 16, 8)
+                fill(W("row2"), 0.0)
+
+        decode(x, 128, "lv", "wv", lambda t: pick(x, 128 * t, l, "xl", 8 * t, 8), halves)
+        back("wv", lambda t, a, b: ts(W(bl, t, 12, 3), W("z4"), a, ADD, b, ADD), idle)
+        spread(bl, ((0, 3), (3, 6), (6, 9), (9, 12)))
+        for b in (2, 3):
+            copy("s", W("ge", C * (b - 2), C * (b - 1)), by(W("de", NS * b, NS * b + NS), W(bl)))
+        for b in (0, 1):
+            tt(W(bt, b, 4 * C, 4), by(W("de", NS * b, NS * b + NS), W(bl)), W("dc", C * b, C * (b + 1)), ADD)
+        for b in (2, 3):
+            tt(W(bt, b, 4 * C, 4), W("ge", C * (b - 2), C * (b - 1)), W("pd%d" % b, 0, C), ADD)
+        quant(n, 0, C, bt, 0)
+        send(2 * turn - 1, n, lambda k: RUN * dests[k], m, OLD)
+        pick(m, OLD + RUN * r, n, "onl", 0, 3)
+        if turn == 1:
+            merge_list(fl, row, ml, [
+                lambda: pick("d2", 128, "d1", "zl", 0, 1), lambda: pick("d2", ST + 128, "d1", "zl", 0, 1),
+                lambda: pick("d2", 2 * ST + 128, "d1", "zl", 0, 1),
+                lambda: (tt(W("dfh"), W("ph", 24, 48), W("ph", 0, 24), SUB), table_a("lh", "wh")),
+                lambda: (ts(W("lh", 48, 72), W("dfh"), float(NS), ADD), table_d("lh", "wh")),
+                lambda: quant("qv", 0, 128, "vt", 0)])
+        else:
+            def visited():
+                copy("v", W("pd"), W(bl))
+                for h in range(N):
+                    dma("y", hbm(T.dl[16 * h:16 * h + 16, :]), W("pd", 3 * h, 3 * h + 3, 1, 0, 16), "out1")
+            merge_list(fl, row, ml, [visited])
+
+    banks = ("pa0", "pb0", "pf1")
+    for t in range(NT):
+        pick("d3", 128 * t, "m2", "ml2", 8 * t, 8)
+        mm(banks[t], "qv", 0, "d3", 128 * t, 128)
+    oc = W("d3c")
+    dma("y", hbm(T.oc[:, :]), (oc[0].bitcast(dt.uint8), oc[1]), "out1")
+    for t in range(NT):
+        copy("s" if t == 1 else "v", W("ys", 128 * t, 128 * t + 128), W(banks[t], 0, 128))
+    dma("y", hbm(T.y[:, 0:256]), W("ys", 0, 256), "out1")
+    dma("y", hbm(T.y[:, 256:384]), W("ys", 256, 384), "out1")
+    for k in range(4):
+        dma("s", hbm(T.osc[4 * k:4 * k + 4, :]), W("d3s", 0, None, 1, 32 * k, 32 * k + 4), "out2")
+    for sem in SEMAPHORES:
+        if count.get(sem, 0) > known["g"].get(sem, 0):
+            g.wait_ge(T.sem[sem], count[sem])

@@ -1,13 +1,16 @@
 from concourse.bass import DstId, RemoteDMATransfer
-from concourse.mybir import dt, AluOpType, ActivationFunctionType
+from concourse.mybir import dt, AluOpType, AxisListType, ActivationFunctionType
 
 N = 4
 NT = 3
 NS = 384
 CAP = 16
 RUN = CAP * NT
+FAR = RUN * (N - 1)
+LW = CAP + RUN * N
 ST = 144
 OLD = ST * NT
+HW = OLD + 128 + FAR
 LOW = -9.0e29
 UW = 520
 
@@ -20,24 +23,25 @@ def _pair(name, n):
     SCRATCH[name + "s"] = ("sbuf", [128, n], "uint8")
 
 
-for _n, _w in (("d1", OLD), ("d2", OLD), ("d3", 128 * NT), ("m1", OLD + N * RUN), ("m2", OLD + N * RUN),
-               ("qe", NS), ("qv", 128), ("qu", 512), ("s1", 3 * RUN), ("s2", 3 * RUN), ("l1", N * RUN),
-               ("l2", N * RUN), ("x1", 128 * NT), ("x2", 128 * NT), ("n1", N * RUN), ("n2", N * RUN)):
+for _n, _w in (("d1", HW), ("d2", HW), ("d3", 128 * NT), ("qe", NS), ("qv", 128), ("qu", 512),
+               ("s1", FAR), ("s2", FAR), ("l1", LW), ("l2", LW), ("x1", 128 * NT), ("x2", 128 * NT),
+               ("n1", FAR), ("n2", FAR)):
     _pair(_n, _w)
-for _n, _w in (("xt", 4 * OLD), ("et", 4 * NS), ("vt", 512), ("ut", 2 * UW), ("bt1", 4 * N * RUN), ("bt2", 4 * N * RUN)):
+for _n, _w in (("xt", 4 * OLD), ("et", 4 * NS), ("vt", 512), ("ut", 2 * UW), ("bt1", 4 * LW), ("bt2", 4 * LW),
+               ("bb", 128), ("tr", 128), ("oh", 128), ("cum", 128), ("cd", 128), ("lt", 192)):
     SCRATCH[_n] = ("sbuf", [128, _w], "bfloat16")
 for _n, _w in (("a0", NS), ("a1", NS), ("f2", NS), ("uu", NS), ("ww", NS), ("rr", NS), ("jk", NS), ("wh", 6 * NS),
-               ("wv", 6 * NS), ("de", 4 * NS), ("dc", 2 * N * RUN), ("ge", 2 * N * RUN), ("jj", 2 * NS),
-               ("j16", 128), ("msk", 128), ("rs", 128), ("cd", 128), ("bb", 128), ("tr", 128), ("oh", 128),
-               ("cum", 128), ("j2", 128), ("jid", 128), ("pm", 4), ("c13", 16), ("cx", 24), ("con", 4), ("c1", 4),
-               ("c2", 4), ("z4", 4), ("cj0", 4), ("cj", 4), ("val", 64), ("ct0", 24), ("ct", 24), ("one", 8),
-               ("gg", 64), ("gs2", 64), ("gs1", 64), ("nf", 16), ("row1", 192), ("row2", 192), ("mk", 128),
-               ("rho", 128), ("mx", 24), ("dfv", 24), ("dfh", 24), ("po", 4), ("pd", 12), ("ys", 128 * NT)):
+               ("wv", 6 * NS), ("de", 4 * NS), ("dc", 3 * LW), ("ge", 2 * LW), ("jj", 2 * NS),
+               ("j16", 128), ("msk", 128), ("mt", 128), ("rs", 128), ("j2", 128), ("jid", 128), ("pm", 4), ("c13", 16),
+               ("cx", 24), ("c1", 4), ("c2", 4), ("z4", 8), ("cj0", 4), ("cj", 4), ("val", 64), ("ct0", 24), ("ct", 24),
+               ("one", 8), ("onewh", 8), ("ggwh", 64), ("gs2wh", 64), ("gs1wh", 64), ("onewv", 8), ("ggwv", 64),
+               ("gs2wv", 64), ("gs1wv", 64), ("nf", 16), ("row1", 192), ("row2", 192), ("mk", 128),
+               ("rho", 128), ("mx", 24), ("dfv", 24), ("dfh", 24), ("po", 4), ("pd", 4), ("ys", 128 * NT), ("yw", HW)):
     SCRATCH[_n] = ("sbuf", [128, _w], "float32")
 for _n, _w in (("pi", 4), ("ph", 48), ("pv", 48)):
     SCRATCH[_n] = ("sbuf", [128, _w], "int32")
-for _n, _w in (("lh", 72), ("lv", 72), ("fl1", 16), ("fl2", 16), ("xl", 24), ("onl", 4), ("zl", 2), ("o2", 4),
-               ("o1", 4), ("bl1", 12), ("bl2", 12), ("so", 4), ("ml1", 24), ("ml2", 24)):
+for _n, _w in (("lh", 72), ("lv", 72), ("fl1", 16), ("fl2", 16), ("xl", 24), ("o2wh", 4), ("o1wh", 4), ("o2wv", 4),
+               ("o1wv", 4), ("bl1", 16), ("bl2", 16), ("so", 4), ("zl", 2), ("ml1", 24), ("ml2", 24)):
     SCRATCH[_n] = ("sbuf", [128, _w], "uint16")
 PSUM = ("pa0", "pb0", "pf1", "pf2", "pd0", "pd1", "pd2", "pd3")
 for _n in PSUM:
@@ -47,8 +51,9 @@ SEMAPHORES = (["cv", "cs", "cp", "cg", "dx0", "deh", "dx1", "dx2", "ddup", "dv",
               + ["ac%d" % k for k in range(4)] + ["as%d" % k for k in range(4)])
 
 ADD, SUB, MUL, MAX = AluOpType.add, AluOpType.subtract, AluOpType.mult, AluOpType.max
-EQ, GT, GE = AluOpType.is_equal, AluOpType.is_gt, AluOpType.is_ge
-COPY, SIGN = ActivationFunctionType.Copy, ActivationFunctionType.Sign
+EQ, GT, LT = AluOpType.is_equal, AluOpType.is_gt, AluOpType.is_lt
+ACT = ActivationFunctionType
+COPY, SIGN = ACT.Copy, ACT.Sign
 
 
 def _meet(a, b):
@@ -79,6 +84,12 @@ def rank_program(g, core, T, topo):
 
     def by(win, off):
         return (win[0].indirect(off[0]), win[1] + off[1])
+
+    def raw(view):
+        return (view[0].bitcast(dt.uint8), view[1])
+
+    def after(view, other):
+        return (view[0], view[1] + other[1])
 
     def wait(q, tok):
         sem, val, clock = tok
@@ -141,6 +152,9 @@ def rank_program(g, core, T, topo):
         else:
             op("s", lambda: g.scalar.activation(out[0], in_[0], COPY), [in_], [out])
 
+    def act(out, in_, func, bias=0.0, scale=1.0):
+        op("s", lambda: g.scalar.activation(out[0], in_[0], func, bias=val_of(bias), scale=scale), [in_, bias], [out])
+
     def tt(out, a, b, o):
         op("v", lambda: g.vector.tensor_tensor(out[0], a[0], b[0], o), [a, b], [out])
 
@@ -155,6 +169,9 @@ def rank_program(g, core, T, topo):
 
     def fill(out, c):
         op("v", lambda: g.vector.memset(out[0], c), [], [out])
+
+    def turn_blocks(out, in_):
+        op("v", lambda: g.vector.transpose(out[0], in_[0]), [in_], [out])
 
     def signs(acc, junk, in_, bias):
         op("s", lambda: g.scalar.activation(junk[0], in_[0], SIGN, bias=bias[0], scale=-1.0, accum_out=acc[0]),
@@ -178,49 +195,58 @@ def rank_program(g, core, T, topo):
         ac, as_, bc, bs = W(a + "c", a0, a0 + 128), W(a + "s", a0, a0 + 128), W(b + "c", b0, b0 + n), W(b + "s", b0, b0 + n)
         op("p", lambda: g.tensor.matmul_mx(o[0], ac[0], as_[0], bc[0], bs[0], True, True), [ac, as_, bc, bs], [o])
 
-    def pickc(dst, c0, src, off, o0, k):
-        o, w, f = W(dst + "c", c0, c0 + 16 * k), W(src + "c"), W(off, o0, o0 + k)
+    def pickc(dst, c0, src, off, o0, k, wide=None):
+        o, w, f = W(dst + "c", c0, c0 + 16 * k), W(src + "c", 0, wide), W(off, o0, o0 + k)
         op("v", lambda: g.vector.tensor_copy(o[0].bitcast(dt.uint32), w[0].bitcast(dt.uint32).indirect(f[0])), [w, f], [o])
 
-    def picks(dst, c0, src, off, o0, k):
-        copy("s", W(dst + "s", c0, c0 + 16 * k), by(W(src + "s"), W(off, o0, o0 + k)))
+    def picks(q, dst, c0, src, off, o0, k, wide=None):
+        copy(q, W(dst + "s", c0, c0 + 16 * k), by(W(src + "s", 0, wide), W(off, o0, o0 + k)))
 
-    def pick(dst, c0, src, off, o0, k):
-        pickc(dst, c0, src, off, o0, k)
-        picks(dst, c0, src, off, o0, k)
+    def pick(dst, c0, src, off, o0, k, wide=None):
+        pickc(dst, c0, src, off, o0, k, wide)
+        picks("s", dst, c0, src, off, o0, k, wide)
 
-    dests = [(r + 1 + k) % N for k in range(N)]
+    def weave(*chains):
+        chains = [list(c) for c in chains]
+        while any(chains):
+            for c in chains:
+                if c:
+                    c.pop(0)()
+
+    ring = [(r + j) % N for j in range(N)]
+    seat = (0, 1, 3, 2)
+    twice = [ring[seat[k // 2]] for k in range(2 * N)]
 
     def engines_of(a, b, k, part):
         e = topo.engines(T.cores[a], T.cores[b])
+        e = e[0::2] + e[1::2]
         h, f = len(e) // 2, len(e) // 4
         return ((e[:h], e[h:h + f], e[h + f:]), (e[h:], e[:f], e[f:h]))[part][k]
 
-    def send(phase, src, at, dst, base):
-        for part, tag, sem in ((0, "c", "ac%d" % phase), (1, "s", "as%d" % phase)):
+    def send(phase, src, dst, base, parts):
+        for part, tag in enumerate(parts):
+            sem = "a%s%d" % (tag, phase)
             moves, reads = [], []
-            for k in range(N - 1):
-                d = dests[k]
+            for j in range(1, N):
+                d = ring[j]
                 rid, pid, _ = topo.addr(T.cores[d])
-                a = W(src + tag, at(k), at(k) + RUN)
-                b = W(dst + tag, base + RUN * r, base + RUN * (r + 1))
+                a = W(src + tag, RUN * (j - 1), RUN * j)
+                b = W(dst + tag, base + RUN * (N - j - 1), base + RUN * (N - j))
                 reads = reads + a[1]
-                m = sum(1 << e for e in engines_of(r, d, k, part))
+                m = sum(1 << e for e in engines_of(r, d, j - 1, part))
                 moves.append(RemoteDMATransfer(
                     dst_ids=[DstId(rid=rid, pnc=pid)], dma_engine_mask=m, remote_sem=T.sem[sem],
-                    src=a[0].bitcast(dt.uint8) if part == 0 else a[0], dst=b[0].bitcast(dt.uint8) if part == 0 else b[0]))
-                count["loc"] = count.get("loc", 0) + len(engines_of(r, d, k, part))
+                    src=raw(a)[0] if tag == "c" else a[0], dst=raw(b)[0] if tag == "c" else b[0]))
+                count["loc"] = count.get("loc", 0) + len(engines_of(r, d, j - 1, part))
             order("g", reads, [])
             g.remote_dma_fused(moves, local_sem=T.sem.loc)
-            total = sum(len(engines_of((r - 1 - k) % N, r, k, part)) for k in range(N - 1))
+            total = sum(len(engines_of((r - j) % N, r, j - 1, part)) for j in range(1, N))
             count[sem] = total
-            for h in range(N):
-                if h != r:
-                    note("far", [], W(dst + tag, base + RUN * h, base + RUN * (h + 1))[1], (sem, total, {}))
+            note("far", [], W(dst + tag, base, base + FAR)[1], (sem, total, {}))
 
     PM, PF, IB = W("pm", 0, 1), W("pm", 1, 2), W("pm", 2, 3)
-    H, G = NS // 2, 256
-    C = N * RUN
+    G = 256
+    A = CAP + RUN
 
     dma("y", W("xt", 0, 512), hbm(T.x[:, 0:512]), "dx0")
     dma("s", W("et", 0, 4 * G), hbm(T.e[:, 0:4 * G]), "del")
@@ -229,257 +255,316 @@ def rank_program(g, core, T, topo):
     dma("s", W("ph", 24, 48), hbm(T.pb[:, :]), "dp", 2)
     for t in (1, 2):
         dma("y", W("xt", 4 * ST * t, 4 * ST * t + 512), hbm(T.x[:, 512 * t:512 * t + 512]), "dx%d" % t)
-    for h in range(N):
-        for u in range(2):
-            p0 = 32 * h + 16 * u
-            dma("y", W("pv", 0, 24, 1, p0, p0 + 16), hbm(T.pa[16 * h:16 * h + 16, :]), "ddup", 4 * N)
-            dma("y", W("pv", 24, 48, 1, p0, p0 + 16), hbm(T.pb[16 * h:16 * h + 16, :]), "ddup", 4 * N)
     dma("y", W("vt"), hbm(T.v[:, :]), "dv")
+    runs = [[0, 1]]
+    for k in range(1, 2 * N):
+        if twice[k] == twice[k - 1] + 1:
+            runs[-1][1] += 1
+        else:
+            runs.append([k, 1])
+    for k, m in runs:
+        dma("y", W("pv", 0, 48, 1, 16 * k, 16 * (k + m)), W("ph", 0, 48, 1, 16 * twice[k], 16 * (twice[k] + m)),
+            "ddup", len(runs))
 
     iota(W("pi", 0, 1), [[0, 1]], 0, 1, True)
     iota(W("jid"), [[1, 128]], 0)
-    iota(W("c13", 0, 9), [[0, 3], [2 * ST, 3]], 128)
-    iota(W("c13", 9, 14), [[2 * ST, 5]], 128 - 2 * ST)
-    iota(W("cx"), [[16, NT], [RUN, N], [0, 2]], 0)
     iota(W("j16"), [[0, 8], [1, 16]], 0)
-    iota(W("con", 0, 3), [[16, 3]], RUN * r)
-    iota(W("c1"), [[NS, 4]], 0)
-    iota(W("c2"), [[-2 * NS, 2], [NS, 2]], 4 * NS)
     iota(W("cj0"), [[16, 4]], 0)
     iota(W("ct0"), [[128, NT], [16, 8]], 0)
+    iota(W("c13", 0, 15), [[0, 5], [2 * ST, 3]], 128)
+    for t in range(NT):
+        for q in (0, 2):
+            iota(W("cx", 8 * t + 2 * q, 8 * t + 2 * q + 4), [[RUN * (seat[q + 1] - seat[q]), 2], [0, 2]],
+                 CAP + 16 * t + RUN * seat[q])
+    iota(W("c1"), [[NS, 4]], 0)
+    iota(W("c2"), [[-2 * NS, 2], [NS, 2]], 4 * NS)
+    iota(W("z4"), [[0, 8]], 0)
     iota(W("jj"), [[1, 2 * NS]], -NS)
+    iota(W("val", 0, 16), [[1, 16]], OLD + CAP)
+    iota(W("val", 16, 64), [[RUN, N - 1], [1, 16]], OLD + 128)
+    iota(W("row1"), [[0, 192]], 0)
     fill(W("ut"), 0.0)
     for t in range(NT):
         fill(W("xt", 4 * (ST * t + 128), 4 * (ST * t + 130)), 0.0)
     copy("v", PF, W("pi", 0, 1))
     ts(W("pi", 1, 2), W("pi", 0, 1), 15, AluOpType.bitwise_and)
-    fill(W("z4"), 0.0)
-    fill(W("zl"), 128)
+    fill(W("bl1"), 0)
+    for q in range(N):
+        fill(W("cd", 32 * q, 32 * q + 32), float(ring[seat[q]]))
+    copy("v", PM, W("pi", 1, 2))
     for u in range(2):
         ts(W("ut", UW * u + 2 + u, UW * u + 514, 4), W("jid"), PF, EQ, 0.5, MUL)
-    copy("v", PM, W("pi", 1, 2))
-    for k in range(N):
-        fill(W("cd", 32 * k, 32 * k + 32), float(dests[k]))
     ts(IB, PM, 0.5, ADD)
     for b in range(4):
         quant_at("qu", 128 * b, 128, "ut", UW * (b % 2) + (2 if b < 2 else 0))
+    act(W("mt"), W("j16"), ACT.Abs, PM, -1.0)
+    act(W("rs"), W("j16"), SIGN)
+    act(W("cj"), W("cj0"), ACT.Identity, PM)
+    act(W("ct"), W("ct0"), ACT.Identity, PM)
+    act(W("msk"), W("mt"), ACT.Relu, 1.0, -1.0)
 
-    def decode(x, stride, lst, w, prep, extra=None, tail=None, late=False):
-        cut = G if late else 224
-        prep(0)
-        mm("pa0", x, 0, "qe", 0, cut)
-        mm("pb0", x, 0, "qe", cut, NS - cut)
-        if not late:
-            prep(1)
-            mm("pf1", x, stride, "qe", 0, NS)
-            prep(2)
-            mm("pf2", x, 2 * stride, "qe", 0, NS)
-        copy("v" if late else "s", W("a0", 0, cut), W("pa0", 0, cut))
-        copy("s" if late else "v", W("a0", cut, NS), W("pb0", 0, NS - cut))
-        copy("s", W(w, 128, NS), by(W("a0"), W(lst, 8, 24)))
-        copy("v", W(w, 0, 128), by(W("a0"), W(lst, 0, 8)))
-        if late:
-            prep(1)
-            mm("pf1", x, stride, "qe", 0, NS)
-        tt(W(w, NS, NS + 128), by(W("a0"), W(lst, 24, 32)), W(w, 0, 128), MAX)
-        if late:
-            prep(2)
-            mm("pf2", x, 2 * stride, "qe", 0, NS)
-        tt(W(w, NS + 128, 2 * NS), by(W("a0"), W(lst, 32, 48)), W(w, 128, NS), MAX)
-        tt(W("a1", 0, 128), W(w, NS, NS + 128), W("pf1", 0, 128), ADD)
-        tt(W("a1", 128, NS), W(w, NS + 128, 2 * NS), W("pf1", 128, NS), ADD)
+    def steps(lst, w, early, mid, tail):
+        def some(which, c0, c1):
+            return W(lst, 24 * which + c0 // 16, 24 * which + c1 // 16)
+
+        def first(q, c0, c1):
+            copy(q, W(w, c0, c1), by(W("a0"), some(0, c0, c1)))
+
+        def larger(c0, c1):
+            tt(W(w, NS + c0, NS + c1), by(W("a0"), some(1, c0, c1)), W(w, c0, c1), MAX)
+        first("s", 128, 320)
+        first("v", 0, 64)
+        first("v", 64, 128)
+        first("s", 320, NS)
+        early(0)
+        larger(0, 64)
+        larger(64, 128)
+        early(1)
+        larger(128, 320)
+        larger(320, NS)
+        for c0, c1 in ((0, 128), (128, 320), (320, NS)):
+            tt(W("a1", c0, c1), W(w, NS + c0, NS + c1), W("pf1", c0, c1), ADD)
         copy("s", W("f2"), W("pf2", 0, NS))
-        if extra is not None:
-            extra()
-        copy("s", W(w, 4 * NS, 4 * NS + H), by(W("a1"), W(lst, 0, 12)))
-        copy("s", W(w, 4 * NS + H, 5 * NS), by(W("a1"), W(lst, 12, 24)))
+        mid()
+        for c0, c1 in ((0, 160), (160, 320)):
+            copy("s", W(w, 4 * NS + c0, 4 * NS + c1), by(W("a1"), some(0, c0, c1)))
         if tail is None:
-            copy("s", W(w, 5 * NS, 6 * NS), by(W("a1"), W(lst, 24, 48)))
+            copy("s", W(w, 4 * NS + 320, 5 * NS), by(W("a1"), some(0, 320, NS)))
+            copy("s", W(w, 5 * NS, 6 * NS), by(W("a1"), some(1, 0, NS)))
         else:
             tail()
-        tt(W("ww"), by(W("a1"), W(lst, 24, 48)), W("f2"), ADD)
-        tt(W("uu", 0, H), W(w, 4 * NS, 4 * NS + H), W("pf2", 0, H), ADD)
-        tt(W("uu", H, NS), W(w, 4 * NS + H, 5 * NS), W("pf2", H, NS), ADD)
+        tt(W("ww"), by(W("a1"), some(1, 0, NS)), W("f2"), ADD)
+        tt(W("uu", 320, NS), by(W("a1"), some(0, 320, NS)), W("f2", 320, NS), ADD)
+        for c0, c1 in ((0, 160), (160, 320)):
+            tt(W("uu", c0, c1), W(w, 4 * NS + c0, 4 * NS + c1), W("pf2", c0, c1), ADD)
         scan(W("rr"), W("uu"), W("ww"), LOW, MAX, MAX)
 
-    def spread(name, blocks):
-        for a in range(4):
-            b = a ^ 1
-            copy("v", W(name, blocks[a][0], blocks[a][1], 1, 32 * b, 32 * b + 32),
-                 W(name, blocks[a][0], blocks[a][1], 1, 32 * a, 32 * a + 32))
-        copy("v", W(name, blocks[0][0], blocks[1][1], 1, 64, 128), W(name, blocks[0][0], blocks[1][1], 1, 0, 64))
-        copy("v", W(name, blocks[2][0], blocks[3][1], 1, 0, 64), W(name, blocks[2][0], blocks[3][1], 1, 64, 128))
+    def decode(x, stride, src, off, lst, w, mid):
+        for t in range(NT):
+            picks("s", x, stride * t, src, off, 8 * t, 8)
+        pickc(x, 0, src, off, 0, 8)
+        mm("pa0", x, 0, "qe", 0, G)
+        mm("pb0", x, 0, "qe", G, NS - G)
+        for t in (1, 2):
+            pickc(x, stride * t, src, off, 8 * t, 8)
+            mm("pf%d" % t, x, stride * t, "qe", 0, NS)
+        copy("s", W("a0", 0, G), W("pa0", 0, G))
+        copy("v", W("a0", G, NS), W("pb0", 0, NS - G))
+        steps(lst, w, lambda k: None, mid, None)
 
-    def admit(fl):
-        top = W("rr", NS - 1, NS)
-        signs(W("one", 0, 1), W("j2", 0, 3), W("rr", NS // N - 1, NS - 1, NS // N), top)
+    def keep(b):
+        copy("s", W("de", NS * b, NS * b + NS), W("pd%d" % b, 0, NS))
+
+    def decode_first():
+        quant("d1", 0, 130, "xt", 0)
+        quant("qe", 0, G, "et", 0)
+        quant("qe", G, NS - G, "et", G)
+        mm("pa0", "d1", 0, "qe", 0, G)
+        mm("pb0", "d1", 0, "qe", G, NS - G)
+        copy("v", W("a0", 0, G), W("pa0", 0, G))
+        copy("v", W("lh", 0, 48), W("ph"))
+        copy("s", W("a0", G, NS), W("pb0", 0, NS - G))
+
+        def early(k):
+            quant("d1", ST * (k + 1), 130, "xt", ST * (k + 1))
+            mm("pf%d" % (k + 1), "d1", ST * (k + 1), "qe", 0, NS)
+            if k == 1:
+                for b in range(4):
+                    mm("pd%d" % b, "qu", 128 * b, "qe", 0, NS)
+        steps("lh", "wh", early, lambda: None, lambda: keep(0))
+
+    def move(q, name, c0, c1, src, dst, tall=32):
+        copy(q, W(name, c0, c1, 1, dst, dst + tall), W(name, c0, c1, 1, src, src + tall))
+
+    HALVES = ((0, 0, 0), (1, 64, 0), (1, 64, 64), (0, 0, 64))
+
+    def beside(name):
+        for a in (0, 64):
+            move("v", name, 4, 10, a + 32, a)
+            move("v", name, 10, 13, a, a + 32)
+
+    def beside_own(name):
+        return [lambda a=a: move("v", name, 0, 4, a, a + 32) for a in (0, 64)]
+
+    def admit(fl, side):
+        def gap(k):
+            for _ in range(k):
+                if side:
+                    side.pop(0)()
+        signs(W("one", 0, 1), W("j2", 0, 3), W("rr", NS // N - 1, NS - 1, NS // N), W("rr", NS - 1, NS))
+        gap(1)
         ts(W("bb"), W("cd"), W("one", 0, 1), EQ)
-        op("v", lambda: g.vector.transpose(W("tr")[0], W("bb")[0]), [W("bb")], [W("tr")])
-        for a in range(4):
-            for k in range(4):
-                copy("v" if (a + k) % 2 == 0 else "s", W("oh", 32 * a, 32 * a + 32, 1, 32 * k, 32 * k + 32),
-                     W("tr", 32 * k, 32 * k + 32, 1, 32 * a, 32 * a + 32))
+        turn_blocks(W("oh"), W("bb"))
+        turn_blocks(W("tr"), W("bb"))
+        gap(1)
+        for i, (a, k) in enumerate([(a, k) for a in range(N) for k in range(N) if a != k]):
+            copy("vs"[i % 2], W("oh", 32 * a, 32 * a + 32, 1, 32 * k, 32 * k + 32),
+                 W("tr", 32 * k, 32 * k + 32, 1, 32 * a, 32 * a + 32))
+        gap(2)
         scan(W("cum"), W("oh"), W("oh"), 0.0, ADD, MAX)
         signs(W("one", 1, 2), W("j2"), W("cum"), IB)
-        ts(W(fl, 0, 14), W("c13", 0, 14), W("one", 1, 2), ADD, 0.5, MUL)
-        spread(fl, ((0, 3), (3, 6), (6, 9), (10, 13)))
+        gap(2)
+        for k, a, b in HALVES:
+            c0, c1 = ((0, 7), (7, 13))[k]
+            ts(W(fl, c0, c1, 1, b, b + 64), W("c13", c0 + 2, c1 + 2, 1, a, a + 64), W("one", 1, 2, 1, a, a + 64), ADD,
+               0.5, MUL)
+        gap(1)
+        beside(fl)
+        gap(1)
 
-    def back(w, put, meanwhile):
-        s2 = W("one", 2, 3)
-        signs(s2, W("jk"), W("rr"), W("rr", NS - 1, NS))
-        meanwhile()
-        ts(W("o2"), W("c2"), s2, ADD)
-        for t, off, gs in ((2, "o2", "gs2"), (1, "o1", "gs1")):
-            tt(W("gg"), by(W(w), W(off)), W("msk", 0, 64), MUL)
-            if t == 2:
-                put(2, s2, 0.0)
-            else:
-                put(1, W("gs2", 47, 48), W("one", 5, 6))
-            scan(W(gs), W("rs", 0, 64), W("gg"), 0.0, MUL, ADD)
-            dd = W("one", 3 + t, 4 + t)
-            ts(dd, W(gs, 31, 32), W(gs, 15, 16), GT, W(gs, 63, 64), MUL)
-            if t == 2:
-                ts(W("o1"), W("c1"), W(gs, 47, 48), ADD, dd, ADD)
-        put(0, W("gs1", 47, 48), W("one", 4, 5))
+    def back(w, put, cut):
+        one, gg, gs2, gs1, o2, o1 = (c + w for c in ("one", "gg", "gs2", "gs1", "o2", "o1"))
+        s2, top = W(one, 2, 3), W("rr", NS - 1, NS)
+        low = W(one, 6, 7) if cut else 0.0
+        calls = [lambda: signs(s2, W("jk", cut, NS), W("rr", cut, NS), top)]
+        if cut:
+            calls += [lambda: ts(W("lt", 0, cut), W("rr", 0, cut), top, LT),
+                      lambda: op("v", lambda: g.vector.tensor_reduce(low[0], W("lt", 0, cut)[0], AxisListType.X, ADD),
+                                 [W("lt", 0, cut)], [low])]
+        calls += [
+            lambda: ts(W(o2), W("c2"), s2, ADD, low, ADD),
+            lambda: tt(W(gg), by(W(w), W(o2)), W("msk", 0, 64), MUL),
+            lambda: put(2, s2, low),
+            lambda: scan(W(gs2), W("rs", 0, 64), W(gg), 0.0, MUL, ADD),
+            lambda: ts(W(one, 5, 6), W(gs2, 31, 32), W(gs2, 15, 16), GT, W(gs2, 63, 64), MUL),
+            lambda: ts(W(o1), W("c1"), W(gs2, 47, 48), ADD, W(one, 5, 6), ADD),
+            lambda: tt(W(gg), by(W(w), W(o1)), W("msk", 0, 64), MUL),
+            lambda: put(1, W(gs2, 47, 48), W(one, 5, 6)),
+            lambda: scan(W(gs1), W("rs", 0, 64), W(gg), 0.0, MUL, ADD),
+            lambda: ts(W(one, 4, 5), W(gs1, 31, 32), W(gs1, 15, 16), GT, W(gs1, 63, 64), MUL),
+            lambda: put(0, W(gs1, 47, 48), W(one, 4, 5))]
+        return calls
 
-    def merge_list(fl, row, ml, between):
-        def gap():
-            if between:
-                between.pop(0)()
-        ts(W("nf", 4, 7), W(fl, 0, 9, 3), -127.0, ADD, 0.0, MAX)
-        ts(W("nf", 7, 8), W(fl, 10, 11), -127.0, ADD, 0.0, MAX)
-        copy("v", W("nf", 0, 3), W(fl, 0, 9, 3))
-        copy("v", W("nf", 3, 4), W(fl, 10, 11))
-        tt(W("nf", 8, 12), W("nf", 4, 8), W("cj"), MUL)
-        gap()
-        tt(W("nf", 12, 16), W("nf", 8, 12), W("nf", 0, 4), ADD)
-        gap()
-        copy("v", W("so"), W("nf", 12, 16))
-        gap()
+    def places(fl):
+        f = W(fl, 1, 13, 3)
+        return [lambda: ts(W("nf", 4, 8), f, 128.0, EQ),
+                lambda: copy("v", W("nf", 0, 4), f),
+                lambda: tt(W("nf", 8, 12), W("nf", 4, 8), W("cj"), MUL),
+                lambda: tt(W("nf", 12, 16), W("nf", 8, 12), W("nf", 0, 4), ADD),
+                lambda: copy("v", W("so"), W("nf", 12, 16))]
+
+    def merge_list(row, ml):
         win = W(row)
-        op("v", lambda: g.vector.tensor_copy(win[0].indirect(W("so")[0]), W("val")[0]), [W("so"), W("val")], [win])
-        gap()
-        tt(W("mk"), W(row, 0, 128), W("msk"), MUL)
-        gap()
-        scan(W("rho"), W("rs"), W("mk"), 0.0, MUL, ADD)
-        gap()
-        for t in range(NT):
-            tt(W("mx", 8 * t, 8 * t + 8), W("rho", 15, 128, 16), W("ct", 8 * t, 8 * t + 8), MAX)
-        for t in range(NT):
-            ts(W(ml, 8 * t, 8 * t + 8), W("mx", 8 * t, 8 * t + 8), float(16 * t), ADD)
-        while between:
-            gap()
+        return ([lambda: op("v", lambda: g.vector.tensor_copy(win[0].indirect(W("so")[0]), W("val")[0]),
+                            [W("so"), W("val")], [win]),
+                 lambda: tt(W("mk"), W(row, 0, 128), W("msk"), MUL),
+                 lambda: scan(W("rho"), W("rs"), W("mk"), 0.0, MUL, ADD)]
+                + [lambda t=t: tt(W("mx", 8 * t, 8 * t + 8), W("rho", 15, 128, 16), W("ct", 8 * t, 8 * t + 8), MAX)
+                   for t in range(NT)]
+                + [lambda t=t: ts(W(ml, 8 * t, 8 * t + 8), W("mx", 8 * t, 8 * t + 8), float(16 * t), ADD)
+                   for t in range(NT)])
 
-    def table_a(lst, w):
-        copy("s", W(w, 2 * NS, 3 * NS), by(W("jj", NS, 2 * NS), W(lst, 0, 24)))
+    def tables(lst, w, src, df):
+        return [lambda: tt(W(df), W(src, 24, 48), W(src, 0, 24), SUB),
+                lambda: copy("s", W(w, 2 * NS, 3 * NS), by(W("jj", NS, 2 * NS), W(lst, 0, 24))),
+                lambda: ts(W(lst, 48, 72), W(df), float(NS), ADD),
+                lambda: copy("s", W(w, 3 * NS, 4 * NS), by(W("jj"), W(lst, 48, 72)))]
 
-    def table_d(lst, w):
-        copy("s", W(w, 3 * NS, 4 * NS), by(W("jj"), W(lst, 48, 72)))
+    def blend(bl, k0, k1, cut, bt):
+        def picked(b, a, z):
+            return by(W("de", NS * b, NS * b + NS), W(bl, a, z))
 
-    def first(t):
-        if t == 0:
-            quant("d1", 0, 130, "xt", 0)
-            quant("qe", 0, G, "et", 0)
-            quant("qe", G, NS - G, "et", G)
-            copy("v", W("lh", 0, 48), W("ph"))
-        else:
-            quant("d1", ST * t, 130, "xt", ST * t)
+        def part(name, at, a, z):
+            return W(name, LW * at + 16 * a, LW * at + 16 * z)
 
-    def unpack_e():
-        for b in range(4):
-            mm("pd%d" % b, "qu", 128 * b, "qe", 0, NS)
-        for b in range(2):
-            copy("s", W("de", NS * b, NS * b + NS), W("pd%d" % b, 0, NS))
+        def out(b, a, z):
+            return W(bt, 64 * a + b, 64 * z, 4)
+        calls = [lambda: copy("s", part("ge", 0, k0, k1), picked(2, k0, k1)),
+                 lambda: copy("s", part("ge", 1, k0, cut), picked(3, k0, cut)),
+                 lambda: tt(out(0, k0, k1), picked(0, k0, k1), part("dc", 0, k0, k1), ADD),
+                 lambda: tt(out(1, k0, k1), picked(1, k0, k1), part("dc", 1, k0, k1), ADD)]
+        if cut < k1:
+            calls += [lambda: tt(out(3, cut, k1), picked(3, cut, k1), part("dc", 2, cut, k1), ADD)]
+        return calls + [lambda: tt(out(2, k0, k1), part("ge", 0, k0, k1), part("pd2", 0, k0, k1), ADD),
+                        lambda: tt(out(3, k0, cut), part("ge", 1, k0, cut), part("pd3", 0, k0, cut), ADD)]
+
+    def product(bank, c0, n):
+        mm(bank, "qv", 0, "d2", c0, n)
+        copy("s", W("yw", c0, c0 + n), W(bank, 0, n))
 
     for turn in (1, 2):
-        d, s, l, x, n, m = ("%s%d" % (c, turn) for c in "dslxnm")
+        d, s, l, x, n = ("%s%d" % (c, turn) for c in "dslxn")
         fl, bl, bt, ml, row = ("%s%d" % (c, turn) for c in ("fl", "bl", "bt", "ml", "row"))
+        home = []
         if turn == 1:
-            decode(d, ST, "lh", "wh", first, None, unpack_e, True)
+            decode_first()
         else:
-            decode(d, ST, "lh", "wh", lambda t: pick("d2", ST * t, "m1", "ml1", 8 * t, 8))
-        admit(fl)
-        pick(s, 0, d, fl, 0, 9)
-        send(2 * turn - 2, s, lambda k: RUN * k, l, 0)
-        pick(l, RUN * r, d, fl, 10, 3)
+            decode("d2", ST, "d1", "ml1", "lh", "wh", lambda: None)
+            home = back("wh", lambda t, a, b: ts(W("po", t, t + 1), W("z4", 0, 1), a, ADD, b, ADD), 0)
+        admit(fl, home)
         if turn == 1:
-            copy("v", W("lv", 0, 48), W("pv"))
-            tt(W("dfv"), W("pv", 24, 48), W("pv", 0, 24), SUB)
-            ts(W("xl"), W("cx"), PM, ADD)
-            ts(W("msk"), W("j16"), PM, EQ)
-            ts(W("lv", 48, 72), W("dfv"), float(NS), ADD)
-            table_a("lv", "wv")
-            table_d("lv", "wv")
-            for b in (2, 3):
-                copy("v", W("de", NS * b, NS * b + NS), W("pd%d" % b, 0, NS))
-            ts(W("rs"), W("j16"), 1.0, GE)
-            ts(W("onl", 0, 3), W("con", 0, 3), PM, ADD)
-            ts(W("cj"), W("cj0"), PM, ADD)
-            ts(W("ct"), W("ct0"), PM, ADD)
-            for k in range(N):
-                ts(W("val", 16 * k, 16 * k + 16), W("j16", 0, 16), float(OLD + RUN * dests[k]), ADD)
-            fill(W("row1"), 0.0)
+            keep(1)
+        pick(s, 0, d, fl, 4, 9, OLD)
+        send(2 * turn - 2, s, l, A, "sc")
+        if turn == 1:
+            iota(W("row2"), [[0, 192]], 0)
+            iota(W("yw"), [[0, HW]], 0)
+        merge = merge_list(row, ml)
+        mine = beside_own(fl) + [lambda: pick(l, 0, d, fl, 0, 4, OLD)] + places(fl) + merge[:1]
+        if turn == 1:
+            weave(mine, [lambda: copy("v", W("lv", 0, 48), W("pv")), lambda: ts(W("xl"), W("cx"), PM, ADD)]
+                  + tables("lv", "wv", "pv", "dfv") + [lambda: fill(W("zl"), 128), lambda: fill(W("bl2"), 0)]
+                  + [lambda t=t: pick("d2", ST * t + 128, "d1", "zl", 0, 1, OLD) for t in range(NT)])
         else:
-            def old_codes():
-                for t in range(2):
-                    pickc("m2", ST * t, "m1", "ml1", 8 * t, 8)
-            back("wh", lambda t, a, b: ts(W("po", t, t + 1), W("z4", 0, 1), a, ADD, b, ADD), old_codes)
-            dma("y", hbm(T.ol[:, :]), W("po", 0, 3), "out1")
+            weave(mine, home)
+            dma("y", hbm(T.ol[:, :]), after(W("po", 0, 3), W("l2c", A, LW)), "out1")
             for t in range(NT):
-                picks("m2", ST * t, "m1", "ml1", 8 * t, 8)
+                product(("pa0", "pb0", "pf1")[t], ST * t, 128)
 
-        def halves():
-            for b in range(4):
-                mm("pd%d" % b, "qu", 128 * b, l, 0, C)
-            for b in range(2):
-                copy("s", W("dc", C * b, C * (b + 1)), W("pd%d" % b, 0, C))
+        def halves(some):
+            for b in some:
+                mm("pd%d" % b, "qu", 128 * b, l, 0, LW)
 
-        def idle():
-            if turn == 1:
-                for t in range(NT):
-                    quant("m1", ST * t, 130, "xt", ST * t)
-            else:
-                pickc("m2", ST * 2, "m1", "ml1", 16, 8)
-                fill(W("row2"), 0.0)
-
-        decode(x, 128, "lv", "wv", lambda t: pick(x, 128 * t, l, "xl", 8 * t, 8), halves)
-        back("wv", lambda t, a, b: ts(W(bl, t, 12, 3), W("z4"), a, ADD, b, ADD), idle)
-        spread(bl, ((0, 3), (3, 6), (6, 9), (9, 12)))
-        for b in (2, 3):
-            copy("s", W("ge", C * (b - 2), C * (b - 1)), by(W("de", NS * b, NS * b + NS), W(bl)))
-        for b in (0, 1):
-            tt(W(bt, b, 4 * C, 4), by(W("de", NS * b, NS * b + NS), W(bl)), W("dc", C * b, C * (b + 1)), ADD)
-        for b in (2, 3):
-            tt(W(bt, b, 4 * C, 4), W("ge", C * (b - 2), C * (b - 1)), W("pd%d" % b, 0, C), ADD)
-        quant(n, 0, C, bt, 0)
-        send(2 * turn - 1, n, lambda k: RUN * dests[k], m, OLD)
-        pick(m, OLD + RUN * r, n, "onl", 0, 3)
+        decode(x, 128, l, "xl", "lv", "wv", lambda: halves(range(2 * turn)))
+        path = back("wv", lambda t, a, b: ts(W(bl, 1 + t, 16, 3), W("z4", 0, 5), a, ADD, b, ADD), 64)
+        path[0]()
+        for b in range(2):
+            copy("s", W("dc", LW * b, LW * (b + 1)), W("pd%d" % b, 0, LW))
         if turn == 1:
-            merge_list(fl, row, ml, [
-                lambda: pick("d2", 128, "d1", "zl", 0, 1), lambda: pick("d2", ST + 128, "d1", "zl", 0, 1),
-                lambda: pick("d2", 2 * ST + 128, "d1", "zl", 0, 1),
-                lambda: (tt(W("dfh"), W("ph", 24, 48), W("ph", 0, 24), SUB), table_a("lh", "wh")),
-                lambda: (ts(W("lh", 48, 72), W("dfh"), float(NS), ADD), table_d("lh", "wh")),
-                lambda: quant("qv", 0, 128, "vt", 0)])
+            for b in (2, 3):
+                keep(b)
+                halves([b])
+        copy("s", W("dc", 2 * LW + 160, 3 * LW), W("pd3", 160, LW))
+        swap = [lambda: move("v", bl, 7, 13, 64, 0, 64), lambda: move("v", bl, 0, 7, 0, 64, 64)]
+        fit = {1: merge[1:2], 3: merge[2:3], 6: merge[3:6], 7: merge[6:9], 11: swap}
+        for k in range(1, len(path) - 1):
+            path[k]()
+            weave(fit.get(k, []))
+        for k, a, b in HALVES:
+            ts(W(bl, 1 + 6 * k, 7 + 6 * k, 3, b, b + 64), W("z4", 0, 2, 1, a, a + 64), W("gs1wv", 47, 48, 1, a, a + 64),
+               ADD, W("onewv", 4, 5, 1, a, a + 64), ADD)
+        if turn == 2:
+            ts(W(bl, 13, 14), W("z4", 0, 1), W("gs1wv", 47, 48), ADD, W("onewv", 4, 5), ADD)
+        beside(bl)
+        weave(beside_own(bl))
+        weave(blend(bl, 4, 13, 10, bt))
+        quant(n, 0, FAR, bt, A)
+        send(2 * turn - 1, n, d, OLD + 128, "sc" if turn == 1 else "cs")
+        mine = blend(bl, 0, 4, 4, bt) + [lambda: quant(d, OLD, 128, bt, 0)]
+        if turn == 1:
+            weave(mine, tables("lh", "wh", "ph", "dfh") + [lambda: quant("qv", 0, 128, "vt", 0)])
         else:
-            def visited():
-                copy("v", W("pd"), W(bl))
-                for h in range(N):
-                    dma("y", hbm(T.dl[16 * h:16 * h + 16, :]), W("pd", 3 * h, 3 * h + 3, 1, 0, 16), "out1")
-            merge_list(fl, row, ml, [visited])
+            copy("v", W("pd", 0, 3), W(bl, 13, 16))
+            q = 0
+            while q < N:
+                m = 2 if q + 1 < N and twice[2 * q + 2] == twice[2 * q] + 1 else 1
+                dma("y", hbm(T.dl[16 * twice[2 * q]:16 * (twice[2 * q] + m), :]),
+                    W("pd", 0, 3, 1, 32 * q + 16, 32 * q + 16 * (m + 1)), "out1")
+                q += m
+            weave(mine)
 
-    banks = ("pa0", "pb0", "pf1")
-    for t in range(NT):
-        pick("d3", 128 * t, "m2", "ml2", 8 * t, 8)
-        mm(banks[t], "qv", 0, "d3", 128 * t, 128)
-    oc = W("d3c")
-    dma("y", hbm(T.oc[:, :]), (oc[0].bitcast(dt.uint8), oc[1]), "out1")
-    for t in range(NT):
-        copy("s" if t == 1 else "v", W("ys", 128 * t, 128 * t + 128), W(banks[t], 0, 128))
-    dma("y", hbm(T.y[:, 0:256]), W("ys", 0, 256), "out1")
-    dma("y", hbm(T.y[:, 256:384]), W("ys", 256, 384), "out1")
+    product("pa0", OLD, 128)
+    pickc("d3", 0, "d2", "ml2", 0, 16)
+    pickc("d3", 256, "d2", "ml2", 16, 8)
+    dma("y", hbm(T.oc[:, :]), raw(W("d3c")), "out1")
+    picks("s", "d3", 256, "d2", "ml2", 16, 8)
+    product("pb0", OLD + 128, FAR)
+    picks("v", "d3", 0, "d2", "ml2", 0, 16)
+    copy("s", W("ys", 0, 224), by(W("yw"), W("ml2", 0, 14)))
+    copy("v", W("ys", 224, 384), by(W("yw"), W("ml2", 14, 24)))
+    dma("s", hbm(T.y[:, :]), W("ys"), "out2")
     for k in range(4):
-        dma("s", hbm(T.osc[4 * k:4 * k + 4, :]), W("d3s", 0, None, 1, 32 * k, 32 * k + 4), "out2")
+        dma("ys"[k // 3], hbm(T.osc[4 * k:4 * k + 4, :]), W("d3s", 0, None, 1, 32 * k, 32 * k + 4), "out%d" % (1 + k // 3))
     for sem in SEMAPHORES:
         if count.get(sem, 0) > known["g"].get(sem, 0):
             g.wait_ge(T.sem[sem], count[sem])

@@ -25,15 +25,15 @@ def _pair(name, n):
 
 for _n, _w in (("d1", HW), ("d2", HW), ("d3", 128 * NT), ("qe", NS), ("qv", 128), ("qu", 512),
                ("s1", FAR), ("s2", FAR), ("l1", LW), ("l2", LW), ("x1", 128 * NT), ("x2", 128 * NT),
-               ("n1", FAR), ("n2", FAR)):
+               ("n1", FAR), ("n2", FAR), ("u1", 192), ("u2", 192)):
     _pair(_n, _w)
-for _n, _w in (("xt", 4 * OLD), ("et", 4 * NS), ("vt", 512), ("ut", 2 * UW), ("bt1", 4 * LW), ("bt2", 4 * LW),
-               ("bb", 128), ("tr", 128), ("oh", 128), ("cum", 128), ("cd", 128), ("lt", 192)):
+for _n, _w in (("xt", 4 * OLD), ("et", 4 * NS), ("vt", 512), ("ut", 2 * UW), ("bt1", 768), ("bt2", 768),
+               ("bb", 96), ("tr", 96), ("oh", 128), ("cum", 128), ("lt", 64)):
     SCRATCH[_n] = ("sbuf", [128, _w], "bfloat16")
 for _n, _w in (("a0", NS), ("a1", NS), ("f2", NS), ("uu", NS), ("ww", NS), ("rr", NS), ("jk", NS), ("wh", 6 * NS),
-               ("wv", 6 * NS), ("de", 4 * NS), ("dc", 3 * LW), ("ge", 2 * LW), ("jj", 2 * NS),
+               ("wv", 6 * NS), ("de", 4 * NS), ("dc", 576), ("ge", 768), ("jj", 2 * NS), ("cu", 12),
                ("j16", 128), ("msk", 128), ("mt", 128), ("rs", 128), ("j2", 128), ("jid", 128), ("pm", 4), ("c13", 16),
-               ("cx", 24), ("c1", 4), ("c2", 4), ("z4", 8), ("cj0", 4), ("cj", 4), ("val", 64), ("ct0", 24), ("ct", 24),
+               ("cx", 24), ("c1", 4), ("c2", 4), ("zz", 32), ("cj0", 4), ("cj", 4), ("val", 64), ("ct0", 24), ("ct", 24),
                ("one", 8), ("onewh", 8), ("ggwh", 64), ("gs2wh", 64), ("gs1wh", 64), ("onewv", 8), ("ggwv", 64),
                ("gs2wv", 64), ("gs1wv", 64), ("nf", 16), ("row1", 192), ("row2", 192), ("mk", 128),
                ("rho", 128), ("mx", 24), ("dfv", 24), ("dfh", 24), ("po", 4), ("pd", 4), ("ys", 128 * NT), ("yw", HW)):
@@ -41,7 +41,7 @@ for _n, _w in (("a0", NS), ("a1", NS), ("f2", NS), ("uu", NS), ("ww", NS), ("rr"
 for _n, _w in (("pi", 4), ("ph", 48), ("pv", 48)):
     SCRATCH[_n] = ("sbuf", [128, _w], "int32")
 for _n, _w in (("lh", 72), ("lv", 72), ("fl1", 16), ("fl2", 16), ("xl", 24), ("o2wh", 4), ("o1wh", 4), ("o2wv", 4),
-               ("o1wv", 4), ("bl1", 16), ("bl2", 16), ("so", 4), ("zl", 2), ("ml1", 24), ("ml2", 24)):
+               ("o1wv", 4), ("bl1", 18), ("bl2", 18), ("ul", 12), ("so", 4), ("zl", 2), ("ml1", 24), ("ml2", 24)):
     SCRATCH[_n] = ("sbuf", [128, _w], "uint16")
 PSUM = ("pa0", "pb0", "pf1", "pf2", "pd0", "pd1", "pd2", "pd3")
 for _n in PSUM:
@@ -170,7 +170,7 @@ def rank_program(g, core, T, topo):
     def fill(out, c):
         op("v", lambda: g.vector.memset(out[0], c), [], [out])
 
-    def turn_blocks(out, in_):
+    def turn_block(out, in_):
         op("v", lambda: g.vector.transpose(out[0], in_[0]), [in_], [out])
 
     def signs(acc, junk, in_, bias):
@@ -223,8 +223,8 @@ def rank_program(g, core, T, topo):
         h, f = len(e) // 2, len(e) // 4
         return ((e[:h], e[h:h + f], e[h + f:]), (e[h:], e[:f], e[f:h]))[part][k]
 
-    def send(phase, src, dst, base, parts):
-        for part, tag in enumerate(parts):
+    def send(phase, src, dst, base):
+        for part, tag in enumerate("cs"):
             sem = "a%s%d" % (tag, phase)
             moves, reads = [], []
             for j in range(1, N):
@@ -251,8 +251,8 @@ def rank_program(g, core, T, topo):
     dma("y", W("xt", 0, 512), hbm(T.x[:, 0:512]), "dx0")
     dma("s", W("et", 0, 4 * G), hbm(T.e[:, 0:4 * G]), "del")
     dma("y", W("et", 4 * G, 4 * NS), hbm(T.e[:, 4 * G:4 * NS]), "deh")
-    dma("s", W("ph", 0, 24), hbm(T.pa[:, :]), "dp", 2)
-    dma("s", W("ph", 24, 48), hbm(T.pb[:, :]), "dp", 2)
+    dma("y", W("ph", 0, 24), hbm(T.pa[:, :]), "dp", 2)
+    dma("y", W("ph", 24, 48), hbm(T.pb[:, :]), "dp", 2)
     for t in (1, 2):
         dma("y", W("xt", 4 * ST * t, 4 * ST * t + 512), hbm(T.x[:, 512 * t:512 * t + 512]), "dx%d" % t)
     dma("y", W("vt"), hbm(T.v[:, :]), "dv")
@@ -270,33 +270,34 @@ def rank_program(g, core, T, topo):
     iota(W("jid"), [[1, 128]], 0)
     iota(W("j16"), [[0, 8], [1, 16]], 0)
     iota(W("cj0"), [[16, 4]], 0)
-    iota(W("ct0"), [[128, NT], [16, 8]], 0)
+    iota(W("ct0"), [[ST - 1, NT], [16, 8]], 0)
     iota(W("c13", 0, 15), [[0, 5], [2 * ST, 3]], 128)
+    iota(W("zz"), [[0, 32]], 0)
+    iota(W("jj"), [[1, 2 * NS]], -NS)
     for t in range(NT):
         for q in (0, 2):
             iota(W("cx", 8 * t + 2 * q, 8 * t + 2 * q + 4), [[RUN * (seat[q + 1] - seat[q]), 2], [0, 2]],
                  CAP + 16 * t + RUN * seat[q])
+    iota(W("val", 0, 16), [[NT, 16]], OLD + 128 - RUN)
+    iota(W("val", 16, 64), [[RUN, N - 1], [NT, 16]], OLD + 128)
+    iota(W("row1"), [[0, 192]], 0)
+    for t in range(NT):
+        iota(W("cu", 4 * t, 4 * t + 3), [[RUN, N - 1]], A + 16 * t)
+        iota(W("cu", 4 * t + 3, 4 * t + 4), [[0, 1]], CAP + 16 * t)
     iota(W("c1"), [[NS, 4]], 0)
     iota(W("c2"), [[-2 * NS, 2], [NS, 2]], 4 * NS)
-    iota(W("z4"), [[0, 8]], 0)
-    iota(W("jj"), [[1, 2 * NS]], -NS)
-    iota(W("val", 0, 16), [[1, 16]], OLD + CAP)
-    iota(W("val", 16, 64), [[RUN, N - 1], [1, 16]], OLD + 128)
-    iota(W("row1"), [[0, 192]], 0)
     fill(W("ut"), 0.0)
     for t in range(NT):
         fill(W("xt", 4 * (ST * t + 128), 4 * (ST * t + 130)), 0.0)
     copy("v", PF, W("pi", 0, 1))
     ts(W("pi", 1, 2), W("pi", 0, 1), 15, AluOpType.bitwise_and)
-    fill(W("bl1"), 0)
-    for q in range(N):
-        fill(W("cd", 32 * q, 32 * q + 32), float(ring[seat[q]]))
-    copy("v", PM, W("pi", 1, 2))
+    fill(W("zl"), 128)
     for u in range(2):
         ts(W("ut", UW * u + 2 + u, UW * u + 514, 4), W("jid"), PF, EQ, 0.5, MUL)
-    ts(IB, PM, 0.5, ADD)
+    copy("v", PM, W("pi", 1, 2))
     for b in range(4):
         quant_at("qu", 128 * b, 128, "ut", UW * (b % 2) + (2 if b < 2 else 0))
+    ts(IB, PM, 0.5, ADD)
     act(W("mt"), W("j16"), ACT.Abs, PM, -1.0)
     act(W("rs"), W("j16"), SIGN)
     act(W("cj"), W("cj0"), ACT.Identity, PM)
@@ -316,12 +317,9 @@ def rank_program(g, core, T, topo):
         first("v", 0, 64)
         first("v", 64, 128)
         first("s", 320, NS)
-        early(0)
-        larger(0, 64)
-        larger(64, 128)
-        early(1)
-        larger(128, 320)
-        larger(320, NS)
+        early()
+        for c0, c1 in ((0, 64), (64, 128), (128, 320), (320, NS)):
+            larger(c0, c1)
         for c0, c1 in ((0, 128), (128, 320), (320, NS)):
             tt(W("a1", c0, c1), W(w, NS + c0, NS + c1), W("pf1", c0, c1), ADD)
         copy("s", W("f2"), W("pf2", 0, NS))
@@ -339,78 +337,88 @@ def rank_program(g, core, T, topo):
             tt(W("uu", c0, c1), W(w, 4 * NS + c0, 4 * NS + c1), W("pf2", c0, c1), ADD)
         scan(W("rr"), W("uu"), W("ww"), LOW, MAX, MAX)
 
-    def decode(x, stride, src, off, lst, w, mid):
-        for t in range(NT):
-            picks("s", x, stride * t, src, off, 8 * t, 8)
-        pickc(x, 0, src, off, 0, 8)
-        mm("pa0", x, 0, "qe", 0, G)
-        mm("pb0", x, 0, "qe", G, NS - G)
+    def decode(x, stride, src, off, lst, w, mid, idle):
+        pickc(x, 0, src, off, 0, 4)
+        pickc(x, 64, src, off, 4, 4)
+        picks("v", x, 0, src, off, 0, 4)
+        picks("s", x, 64, src, off, 4, 4)
+        cut = 240
+        mm("pa0", x, 0, "qe", 0, cut)
+        mm("pb0", x, 0, "qe", cut, NS - cut)
         for t in (1, 2):
-            pickc(x, stride * t, src, off, 8 * t, 8)
+            pick(x, stride * t, src, off, 8 * t, 8)
             mm("pf%d" % t, x, stride * t, "qe", 0, NS)
-        copy("s", W("a0", 0, G), W("pa0", 0, G))
-        copy("v", W("a0", G, NS), W("pb0", 0, NS - G))
-        steps(lst, w, lambda k: None, mid, None)
+        copy("s", W("a0", 0, cut), W("pa0", 0, cut))
+        idle(0)
+        copy("v", W("a0", cut, NS), W("pb0", 0, NS - cut))
+        idle(1)
+        steps(lst, w, lambda: None, mid, None)
 
     def keep(b):
         copy("s", W("de", NS * b, NS * b + NS), W("pd%d" % b, 0, NS))
 
     def decode_first():
+        def later(t):
+            quant("d1", ST * t, 130, "xt", ST * t)
+            mm("pf%d" % t, "d1", ST * t, "qe", 0, NS)
+            if t == 2:
+                for b in range(4):
+                    mm("pd%d" % b, "qu", 128 * b, "qe", 0, NS)
         quant("d1", 0, 130, "xt", 0)
         quant("qe", 0, G, "et", 0)
         quant("qe", G, NS - G, "et", G)
         mm("pa0", "d1", 0, "qe", 0, G)
         mm("pb0", "d1", 0, "qe", G, NS - G)
-        copy("v", W("a0", 0, G), W("pa0", 0, G))
         copy("v", W("lh", 0, 48), W("ph"))
+        copy("v", W("a0", 0, G), W("pa0", 0, G))
         copy("s", W("a0", G, NS), W("pb0", 0, NS - G))
+        later(1)
+        steps("lh", "wh", lambda: later(2), lambda: None, lambda: keep(0))
 
-        def early(k):
-            quant("d1", ST * (k + 1), 130, "xt", ST * (k + 1))
-            mm("pf%d" % (k + 1), "d1", ST * (k + 1), "qe", 0, NS)
-            if k == 1:
-                for b in range(4):
-                    mm("pd%d" % b, "qu", 128 * b, "qe", 0, NS)
-        steps("lh", "wh", early, lambda: None, lambda: keep(0))
-
-    def move(q, name, c0, c1, src, dst, tall=32):
-        copy(q, W(name, c0, c1, 1, dst, dst + tall), W(name, c0, c1, 1, src, src + tall))
+    def move(name, c0, c1, st, src, dst):
+        copy("v", W(name, c0, c1, st, dst, dst + 32), W(name, c0, c1, st, src, src + 32))
 
     HALVES = ((0, 0, 0), (1, 64, 0), (1, 64, 64), (0, 0, 64))
-
-    def beside(name):
-        for a in (0, 64):
-            move("v", name, 4, 10, a + 32, a)
-            move("v", name, 10, 13, a, a + 32)
-
-    def beside_own(name):
-        return [lambda a=a: move("v", name, 0, 4, a, a + 32) for a in (0, 64)]
 
     def admit(fl, side):
         def gap(k):
             for _ in range(k):
                 if side:
                     side.pop(0)()
-        signs(W("one", 0, 1), W("j2", 0, 3), W("rr", NS // N - 1, NS - 1, NS // N), W("rr", NS - 1, NS))
         gap(1)
-        ts(W("bb"), W("cd"), W("one", 0, 1), EQ)
-        turn_blocks(W("oh"), W("bb"))
-        turn_blocks(W("tr"), W("bb"))
+        part = NS // N
+        for k in range(1, N):
+            ts(W("bb", 32 * k - 32, 32 * k), W("zz"), W("rr", part * k - 1, part * k), ADD, W("rr", NS - 1, NS), LT)
+        for k in range(N - 1):
+            turn_block(W("tr", 32 * k, 32 * k + 32), W("bb", 32 * k, 32 * k + 32))
+        for k in (0, 1, 3, 2):
+            q = twice.index(k) // 2
+            for a in range(N):
+                out = W("oh", 32 * a, 32 * a + 32, 1, 32 * q, 32 * q + 32)
+                if k > 0:
+                    reach = W("tr", 32 * k - 32, 32 * k, 1, 32 * a, 32 * a + 32)
+                if k < N - 1:
+                    past = W("tr", 32 * k, 32 * k + 32, 1, 32 * a, 32 * a + 32)
+                if k == 0:
+                    act(out, past, ACT.Identity, 1.0, -1.0)
+                elif k == N - 1:
+                    copy("s", out, reach)
+                else:
+                    tt(out, reach, past, SUB)
         gap(1)
-        for i, (a, k) in enumerate([(a, k) for a in range(N) for k in range(N) if a != k]):
-            copy("vs"[i % 2], W("oh", 32 * a, 32 * a + 32, 1, 32 * k, 32 * k + 32),
-                 W("tr", 32 * k, 32 * k + 32, 1, 32 * a, 32 * a + 32))
-        gap(2)
         scan(W("cum"), W("oh"), W("oh"), 0.0, ADD, MAX)
         signs(W("one", 1, 2), W("j2"), W("cum"), IB)
-        gap(2)
+        gap(3)
         for k, a, b in HALVES:
             c0, c1 = ((0, 7), (7, 13))[k]
             ts(W(fl, c0, c1, 1, b, b + 64), W("c13", c0 + 2, c1 + 2, 1, a, a + 64), W("one", 1, 2, 1, a, a + 64), ADD,
                0.5, MUL)
         gap(1)
-        beside(fl)
-        gap(1)
+        for a in (0, 64):
+            move(fl, 4, 10, 1, a + 32, a)
+            move(fl, 10, 13, 1, a, a + 32)
+        for a in (0, 64):
+            move(fl, 0, 4, 1, a, a + 32)
 
     def back(w, put, cut):
         one, gg, gs2, gs1, o2, o1 = (c + w for c in ("one", "gg", "gs2", "gs1", "o2", "o1"))
@@ -437,8 +445,7 @@ def rank_program(g, core, T, topo):
 
     def places(fl):
         f = W(fl, 1, 13, 3)
-        return [lambda: ts(W("nf", 4, 8), f, 128.0, EQ),
-                lambda: copy("v", W("nf", 0, 4), f),
+        return [lambda: (ts(W("nf", 4, 8), f, 128.0, EQ), copy("v", W("nf", 0, 4), f)),
                 lambda: tt(W("nf", 8, 12), W("nf", 4, 8), W("cj"), MUL),
                 lambda: tt(W("nf", 12, 16), W("nf", 8, 12), W("nf", 0, 4), ADD),
                 lambda: copy("v", W("so"), W("nf", 12, 16))]
@@ -446,13 +453,12 @@ def rank_program(g, core, T, topo):
     def merge_list(row, ml):
         win = W(row)
         return ([lambda: op("v", lambda: g.vector.tensor_copy(win[0].indirect(W("so")[0]), W("val")[0]),
-                            [W("so"), W("val")], [win]),
-                 lambda: tt(W("mk"), W(row, 0, 128), W("msk"), MUL),
-                 lambda: scan(W("rho"), W("rs"), W("mk"), 0.0, MUL, ADD)]
+                            [W("so"), W("val")], [win])]
+                + [lambda c=c: tt(W("mk", c, c + 64), W(row, c, c + 64), W("msk", 0, 64), MUL) for c in (0, 64)]
+                + [lambda: scan(W("rho"), W("rs"), W("mk"), 0.0, MUL, ADD)]
                 + [lambda t=t: tt(W("mx", 8 * t, 8 * t + 8), W("rho", 15, 128, 16), W("ct", 8 * t, 8 * t + 8), MAX)
                    for t in range(NT)]
-                + [lambda t=t: ts(W(ml, 8 * t, 8 * t + 8), W("mx", 8 * t, 8 * t + 8), float(16 * t), ADD)
-                   for t in range(NT)])
+                + [lambda t=t: ts(W(ml, 8 * t, 8 * t + 8), W("mx", 8 * t, 8 * t + 8), float(t), ADD) for t in range(NT)])
 
     def tables(lst, w, src, df):
         return [lambda: tt(W(df), W(src, 24, 48), W(src, 0, 24), SUB),
@@ -460,108 +466,130 @@ def rank_program(g, core, T, topo):
                 lambda: ts(W(lst, 48, 72), W(df), float(NS), ADD),
                 lambda: copy("s", W(w, 3 * NS, 4 * NS), by(W("jj"), W(lst, 48, 72)))]
 
-    def blend(bl, k0, k1, cut, bt):
-        def picked(b, a, z):
-            return by(W("de", NS * b, NS * b + NS), W(bl, a, z))
+    def blend(bl, t, mine, bt, fused):
+        f = W(bl, 6 * t + 4, 6 * t + 5) if mine else W(bl, 6 * t, 6 * t + 3)
+        c0, c1 = (64 * t + RUN, 64 * t + 64) if mine else (64 * t, 64 * t + RUN)
+        e0, e1 = (4 * FAR, 4 * (FAR + RUN)) if mine else (0, 4 * FAR)
 
-        def part(name, at, a, z):
-            return W(name, LW * at + 16 * a, LW * at + 16 * z)
+        def picked(b):
+            return by(W("de", NS * b, NS * b + NS), f)
 
-        def out(b, a, z):
-            return W(bt, 64 * a + b, 64 * z, 4)
-        calls = [lambda: copy("s", part("ge", 0, k0, k1), picked(2, k0, k1)),
-                 lambda: copy("s", part("ge", 1, k0, cut), picked(3, k0, cut)),
-                 lambda: tt(out(0, k0, k1), picked(0, k0, k1), part("dc", 0, k0, k1), ADD),
-                 lambda: tt(out(1, k0, k1), picked(1, k0, k1), part("dc", 1, k0, k1), ADD)]
-        if cut < k1:
-            calls += [lambda: tt(out(3, cut, k1), picked(3, cut, k1), part("dc", 2, cut, k1), ADD)]
-        return calls + [lambda: tt(out(2, k0, k1), part("ge", 0, k0, k1), part("pd2", 0, k0, k1), ADD),
-                        lambda: tt(out(3, k0, cut), part("ge", 1, k0, cut), part("pd3", 0, k0, cut), ADD)]
+        def part(name, b):
+            return W(name, 192 * b + c0, 192 * b + c1)
+
+        def out(b):
+            return W(bt, e0 + 4 * t + b, e1, 4 * NT)
+        return ([lambda b=b: copy("s", part("ge", b), picked(b)) for b in range(fused, 4)]
+                + [lambda b=b: tt(out(b), picked(b), part("dc", b), ADD) for b in range(fused)]
+                + [lambda b=b: tt(out(b), part("ge", b), W("pd%d" % b, c0, c1), ADD) for b in range(fused, 4)])
 
     def product(bank, c0, n):
         mm(bank, "qv", 0, "d2", c0, n)
         copy("s", W("yw", c0, c0 + n), W(bank, 0, n))
 
+    rows = tables("lh", "wh", "ph", "dfh")
     for turn in (1, 2):
-        d, s, l, x, n = ("%s%d" % (c, turn) for c in "dslxn")
+        d, s, l, x, n, u = ("%s%d" % (c, turn) for c in "dslxnu")
         fl, bl, bt, ml, row = ("%s%d" % (c, turn) for c in ("fl", "bl", "bt", "ml", "row"))
         home = []
         if turn == 1:
             decode_first()
         else:
-            decode("d2", ST, "d1", "ml1", "lh", "wh", lambda: None)
-            home = back("wh", lambda t, a, b: ts(W("po", t, t + 1), W("z4", 0, 1), a, ADD, b, ADD), 0)
+            decode("d2", ST, "d1", "ml1", "lh", "wh", lambda: None, lambda k: None)
+            home = back("wh", lambda t, a, b: ts(W("po", t, t + 1), W("zz", 0, 1), a, ADD, b, ADD), 0)
         admit(fl, home)
         if turn == 1:
             keep(1)
         pick(s, 0, d, fl, 4, 9, OLD)
-        send(2 * turn - 2, s, l, A, "sc")
+        send(2 * turn - 2, s, l, A)
         if turn == 1:
             iota(W("row2"), [[0, 192]], 0)
             iota(W("yw"), [[0, HW]], 0)
         merge = merge_list(row, ml)
-        mine = beside_own(fl) + [lambda: pick(l, 0, d, fl, 0, 4, OLD)] + places(fl) + merge[:1]
+        mine = places(fl) + merge[:1]
         if turn == 1:
-            weave(mine, [lambda: copy("v", W("lv", 0, 48), W("pv")), lambda: ts(W("xl"), W("cx"), PM, ADD)]
-                  + tables("lv", "wv", "pv", "dfv") + [lambda: fill(W("zl"), 128), lambda: fill(W("bl2"), 0)]
+            there = tables("lv", "wv", "pv", "dfv")
+            weave(mine, [lambda: pick(l, 0, d, fl, 0, 4, OLD), lambda: copy("v", W("lv", 0, 48), W("pv")),
+                         lambda: ts(W("xl"), W("cx"), PM, ADD), lambda: ts(W("ul"), W("cu"), PM, ADD), rows[2]],
+                  there[:1] + rows[:1] + there[1:] + [lambda: quant("qv", 0, 128, "vt", 0)]
                   + [lambda t=t: pick("d2", ST * t + 128, "d1", "zl", 0, 1, OLD) for t in range(NT)])
         else:
-            weave(mine, home)
-            dma("y", hbm(T.ol[:, :]), after(W("po", 0, 3), W("l2c", A, LW)), "out1")
+            weave(mine, home, [lambda: pick(l, 0, d, fl, 0, 4, OLD)])
+            dma("y", hbm(T.ol[:, :]), after(W("po", 0, 3), W("l2s", A, LW)), "out1")
             for t in range(NT):
                 product(("pa0", "pb0", "pf1")[t], ST * t, 128)
 
-        def halves(some):
-            for b in some:
-                mm("pd%d" % b, "qu", 128 * b, l, 0, LW)
+        def halves():
+            picks("s", u, 0, l, "ul", 0, 6)
+            picks("s", u, 96, l, "ul", 6, 6)
+            for b in range(2 + turn):
+                if turn == 1 and b == 2:
+                    keep(2)
+                mm("pd%d" % b, "qu", 128 * b, u, 0, 192)
 
-        decode(x, 128, l, "xl", "lv", "wv", lambda: halves(range(2 * turn)))
-        path = back("wv", lambda t, a, b: ts(W(bl, 1 + t, 16, 3), W("z4", 0, 5), a, ADD, b, ADD), 64)
+        decode(x, 128, l, "xl", "lv", "wv", halves, lambda k: pickc(u, 96 * k, l, "ul", 6 * k, 6))
+
+        sums = ((("gs1wv", 47), ("onewv", 4)), (("gs2wv", 47), ("onewv", 5)), (("onewv", 2), ("onewv", 6)))
+
+        def put(t, some=HALVES):
+            (a, i), (b, j) = sums[t]
+            for k, p, q in some:
+                c0, c1, st = (6 * t + 1, 6 * t + 3, 1) if k else (6 * t, 6 * t + 5, 4)
+                ts(W(bl, c0, c1, st, q, q + 64), W("zz", 0, 2, 1, p, p + 64), W(a, i, i + 1, 1, p, p + 64), ADD,
+                   W(b, j, j + 1, 1, p, p + 64), ADD)
+
+        def near(t, some):
+            for a in some:
+                move(bl, 6 * t, 6 * t + 2, 1, a + 32, a)
+                move(bl, 6 * t + 2, 6 * t + 5, 2, a, a + 32)
+
+        path = back("wv", None, 64)
         path[0]()
-        for b in range(2):
-            copy("s", W("dc", LW * b, LW * (b + 1)), W("pd%d" % b, 0, LW))
         if turn == 1:
-            for b in (2, 3):
-                keep(b)
-                halves([b])
-        copy("s", W("dc", 2 * LW + 160, 3 * LW), W("pd3", 160, LW))
-        swap = [lambda: move("v", bl, 7, 13, 64, 0, 64), lambda: move("v", bl, 0, 7, 0, 64, 64)]
-        fit = {1: merge[1:2], 3: merge[2:3], 6: merge[3:6], 7: merge[6:9], 11: swap}
-        for k in range(1, len(path) - 1):
+            keep(3)
+            mm("pd3", "qu", 384, u, 0, 192)
+        for b in range(3):
+            copy("s", W("dc", 192 * b, 192 * (b + 1)), W("pd%d" % b, 0, 192))
+        new = [blend(bl, t, False, bt, 0 if t else 3) for t in range(NT)]
+        fit = {1: merge[1:2], 2: merge[2:3], 3: [lambda: put(2, HALVES[:3])],
+               4: [lambda: put(2, HALVES[3:]), lambda: near(2, [0])], 6: [lambda: near(2, [64])] + new[2][:4],
+               7: merge[3:4], 8: [lambda: put(1)], 9: [lambda: near(1, [0, 64])] + new[1][:4], 11: new[2][4:7],
+               12: new[2][7:] + merge[4:6]}
+        for k in (1, 2, 3, 4, 6, 7, 8, 9, 11, 12):
             path[k]()
             weave(fit.get(k, []))
-        for k, a, b in HALVES:
-            ts(W(bl, 1 + 6 * k, 7 + 6 * k, 3, b, b + 64), W("z4", 0, 2, 1, a, a + 64), W("gs1wv", 47, 48, 1, a, a + 64),
-               ADD, W("onewv", 4, 5, 1, a, a + 64), ADD)
-        if turn == 2:
-            ts(W(bl, 13, 14), W("z4", 0, 1), W("gs1wv", 47, 48), ADD, W("onewv", 4, 5), ADD)
-        beside(bl)
-        weave(beside_own(bl))
-        weave(blend(bl, 4, 13, 10, bt))
-        quant(n, 0, FAR, bt, A)
-        send(2 * turn - 1, n, d, OLD + 128, "sc" if turn == 1 else "cs")
-        mine = blend(bl, 0, 4, 4, bt) + [lambda: quant(d, OLD, 128, bt, 0)]
+        put(0)
+        weave(new[1][4:5])
+        near(0, [0, 64])
+        weave(new[1][5:] + new[0] + merge[6:7])
+        quant(n, 0, FAR, bt, 0)
+        send(2 * turn - 1, n, d, OLD + 128)
+        weave([c for some in zip(*[blend(bl, t, True, bt, 3) for t in range(NT)]) for c in some] + merge[7:])
+        quant(d, OLD, 128, bt, 64)
         if turn == 1:
-            weave(mine, tables("lh", "wh", "ph", "dfh") + [lambda: quant("qv", 0, 128, "vt", 0)])
+            weave(rows[1::2])
         else:
-            copy("v", W("pd", 0, 3), W(bl, 13, 16))
+            for t, ((a, i), (b, j)) in enumerate(sums):
+                ts(W("pd", t, t + 1), W("zz", 0, 1), W(a, i, i + 1), ADD, W(b, j, j + 1), ADD)
             q = 0
             while q < N:
                 m = 2 if q + 1 < N and twice[2 * q + 2] == twice[2 * q] + 1 else 1
                 dma("y", hbm(T.dl[16 * twice[2 * q]:16 * (twice[2 * q] + m), :]),
                     W("pd", 0, 3, 1, 32 * q + 16, 32 * q + 16 * (m + 1)), "out1")
                 q += m
-            weave(mine)
 
     product("pa0", OLD, 128)
-    pickc("d3", 0, "d2", "ml2", 0, 16)
-    pickc("d3", 256, "d2", "ml2", 16, 8)
-    dma("y", hbm(T.oc[:, :]), raw(W("d3c")), "out1")
-    picks("s", "d3", 256, "d2", "ml2", 16, 8)
+    pickc("d3", 0, "d2", "ml2", 0, 8)
+    dma("y", hbm(T.oc[:, 0:512]), raw(W("d3c", 0, 128)), "out1")
+    pickc("d3", 128, "d2", "ml2", 8, 6)
+    pickc("d3", 224, "d2", "ml2", 14, 10)
+    dma("y", hbm(T.oc[:, 512:1536]), raw(W("d3c", 128, 384)), "out1")
+    picks("s", "d3", 224, "d2", "ml2", 14, 10)
     product("pb0", OLD + 128, FAR)
-    picks("v", "d3", 0, "d2", "ml2", 0, 16)
-    copy("s", W("ys", 0, 224), by(W("yw"), W("ml2", 0, 14)))
-    copy("v", W("ys", 224, 384), by(W("yw"), W("ml2", 14, 24)))
+    picks("v", "d3", 0, "d2", "ml2", 0, 8)
+    picks("s", "d3", 128, "d2", "ml2", 8, 6)
+    copy("s", W("ys", 0, 192), by(W("yw"), W("ml2", 0, 12)))
+    copy("v", W("ys", 192, 384), by(W("yw"), W("ml2", 12, 24)))
     dma("s", hbm(T.y[:, :]), W("ys"), "out2")
     for k in range(4):
         dma("ys"[k // 3], hbm(T.osc[4 * k:4 * k + 4, :]), W("d3s", 0, None, 1, 32 * k, 32 * k + 4), "out%d" % (1 + k // 3))

from concourse.bass import DstId, RemoteDMATransfer
from concourse.mybir import dt, AluOpType, AxisListType, ActivationFunctionType

N = 4
NT = 3
NS = 384
CAP = 16
RUN = CAP * NT
FAR = RUN * (N - 1)
LW = CAP + RUN * N
ST = 144
OLD = ST * NT
HW = OLD + 128 + FAR
LOW = -9.0e29
UW = 520

C4 = "float8_e4m3fn_x4"
SCRATCH = {}


def _pair(name, n):
    SCRATCH[name + "c"] = ("sbuf", [128, n], C4)
    SCRATCH[name + "s"] = ("sbuf", [128, n], "uint8")


for _n, _w in (("d1", HW), ("d2", HW), ("d3", 128 * NT), ("qe", NS), ("qv", 128), ("qu", 512),
               ("s1", FAR), ("s2", FAR), ("l1", LW), ("l2", LW), ("x1", 128 * NT), ("x2", 128 * NT),
               ("n1", FAR), ("n2", FAR), ("u1", 192), ("u2", 192)):
    _pair(_n, _w)
for _n, _w in (("xt", 4 * OLD), ("et", 4 * NS), ("vt", 512), ("ut", 2 * UW), ("bt1", 768), ("bt2", 768),
               ("bb", 96), ("tr", 96), ("oh", 128), ("cum", 128), ("lt", 64)):
    SCRATCH[_n] = ("sbuf", [128, _w], "bfloat16")
for _n, _w in (("a0", NS), ("a1", NS), ("f2", NS), ("uu", NS), ("ww", NS), ("rr", NS), ("jk", NS), ("wh", 6 * NS),
               ("wv", 6 * NS), ("de", 4 * NS), ("dc", 576), ("ge", 768), ("jj", 2 * NS), ("cu", 12),
               ("j16", 128), ("msk", 128), ("mt", 128), ("rs", 128), ("j2", 128), ("jid", 128), ("pm", 4), ("c13", 16),
               ("cx", 24), ("c1", 4), ("c2", 4), ("zz", 32), ("cj0", 4), ("cj", 4), ("val", 64), ("ct0", 24), ("ct", 24),
               ("one", 8), ("onewh", 8), ("ggwh", 64), ("gs2wh", 64), ("gs1wh", 64), ("onewv", 8), ("ggwv", 64),
               ("gs2wv", 64), ("gs1wv", 64), ("nf", 16), ("row1", 192), ("row2", 192), ("mk", 128),
               ("rho", 128), ("mx", 24), ("dfv", 24), ("dfh", 24), ("po", 4), ("pd", 4), ("ys", 128 * NT), ("yw", HW)):
    SCRATCH[_n] = ("sbuf", [128, _w], "float32")
for _n, _w in (("pi", 4), ("ph", 48), ("pv", 48)):
    SCRATCH[_n] = ("sbuf", [128, _w], "int32")
for _n, _w in (("lh", 72), ("lv", 72), ("fl1", 16), ("fl2", 16), ("xl", 24), ("o2wh", 4), ("o1wh", 4), ("o2wv", 4),
               ("o1wv", 4), ("bl1", 18), ("bl2", 18), ("ul", 12), ("so", 4), ("zl", 2), ("ml1", 24), ("ml2", 24)):
    SCRATCH[_n] = ("sbuf", [128, _w], "uint16")
PSUM = ("pa0", "pb0", "pf1", "pf2", "pd0", "pd1", "pd2", "pd3")
for _n in PSUM:
    SCRATCH[_n] = ("psum", [128, 512], "float32")

SEMAPHORES = (["cv", "cs", "cp", "cg", "dx0", "deh", "dx1", "dx2", "ddup", "dv", "del", "dp", "loc", "out1", "out2"]
              + ["ac%d" % k for k in range(4)] + ["as%d" % k for k in range(4)])

ADD, SUB, MUL, MAX = AluOpType.add, AluOpType.subtract, AluOpType.mult, AluOpType.max
EQ, GT, LT = AluOpType.is_equal, AluOpType.is_gt, AluOpType.is_lt
ACT = ActivationFunctionType
COPY, SIGN = ACT.Copy, ACT.Sign


def _meet(a, b):
    if a[2] <= b[1] or b[2] <= a[1] or a[4] <= b[3] or b[4] <= a[3]:
        return False
    if a[5] == 1 and b[5] == 1:
        return True
    return len(set(range(a[3], a[4], a[5])) & set(range(b[3], b[4], b[5]))) > 0


def rank_program(g, core, T, topo):
    r = T.rank_of(core)
    if r is None:
        return
    eng = {"v": g.vector, "s": g.scalar, "p": g.tensor, "g": g, "y": g.sync}
    own = {"v": "cv", "s": "cs", "p": "cp", "g": "cg"}
    count = {}
    known = {q: {} for q in eng}
    hist = {}

    def W(name, c0=0, c1=None, st=1, p0=0, p1=128):
        if c1 is None:
            c1 = SCRATCH[name][1][1]
        ap = T[name][p0:p1, c0:c1] if st == 1 else T[name][p0:p1, c0:c1:st]
        if name in PSUM:
            return (ap, [(name, 0, 128, 0, 512, 1)])
        return (ap, [(name, p0, p1, c0, c1, st)])

    def by(win, off):
        return (win[0].indirect(off[0]), win[1] + off[1])

    def raw(view):
        return (view[0].bitcast(dt.uint8), view[1])

    def after(view, other):
        return (view[0], view[1] + other[1])

    def wait(q, tok):
        sem, val, clock = tok
        if known[q].get(sem, 0) >= val:
            return
        eng[q].wait_ge(T.sem[sem], val)
        known[q][sem] = val
        for k in clock:
            if known[q].get(k, 0) < clock[k]:
                known[q][k] = clock[k]

    def order(q, reads, writes):
        need = {}
        for some, wr in ((reads, False), (writes, True)):
            for reg in some:
                for (oreg, owr, oq, tok) in hist.get(reg[0], []):
                    clash = wr or owr or (reg[0] in PSUM and oq != q)
                    if clash and _meet(reg, oreg) and (tok[0] not in need or need[tok[0]][1] < tok[1]):
                        need[tok[0]] = tok
        for k in sorted(need, key=lambda s: s == own.get(q)):
            wait(q, need[k])

    def note(q, reads, writes, tok):
        for reg in reads:
            hist.setdefault(reg[0], []).append((reg, False, q, tok))
        for reg in writes:
            hist.setdefault(reg[0], []).append((reg, True, q, tok))

    def regs(views):
        out = []
        for v in views:
            if isinstance(v, tuple):
                out = out + v[1]
        return out

    def op(q, make, ins, outs):
        reads, writes = regs(ins), regs(outs)
        order(q, reads, writes)
        sem = own[q]
        count[sem] = count.get(sem, 0) + 1
        make().then_inc(T.sem[sem], 1)
        note(q, reads, writes, (sem, count[sem], dict(known[q])))

    def dma(q, out, in_, sem, total=1):
        reads, writes = regs([in_]), regs([out])
        order(q, reads, writes)
        count[sem] = count.get(sem, 0) + 16
        eng[q].dma_start(out[0], in_[0]).then_inc(T.sem[sem], 16)
        note(q, reads, writes, (sem, 16 * total, dict(known[q])))

    def hbm(ap):
        return (ap, [])

    def val_of(s):
        return s[0] if isinstance(s, tuple) else s

    def copy(q, out, in_):
        if q == "v":
            op("v", lambda: g.vector.tensor_copy(out[0], in_[0]), [in_], [out])
        else:
            op("s", lambda: g.scalar.activation(out[0], in_[0], COPY), [in_], [out])

    def act(out, in_, func, bias=0.0, scale=1.0):
        op("s", lambda: g.scalar.activation(out[0], in_[0], func, bias=val_of(bias), scale=scale), [in_, bias], [out])

    def tt(out, a, b, o):
        op("v", lambda: g.vector.tensor_tensor(out[0], a[0], b[0], o), [a, b], [out])

    def ts(out, a, s1, o1, s2=None, o2=None):
        if o2 is None:
            op("v", lambda: g.vector.tensor_scalar(out[0], a[0], val_of(s1), None, o1), [a, s1], [out])
        else:
            op("v", lambda: g.vector.tensor_scalar(out[0], a[0], val_of(s1), val_of(s2), o1, o2), [a, s1, s2], [out])

    def scan(out, a, b, init, o1, o2):
        op("v", lambda: g.vector.tensor_tensor_scan(out[0], a[0], b[0], init, o1, o2), [a, b], [out])

    def fill(out, c):
        op("v", lambda: g.vector.memset(out[0], c), [], [out])

    def turn_block(out, in_):
        op("v", lambda: g.vector.transpose(out[0], in_[0]), [in_], [out])

    def signs(acc, junk, in_, bias):
        op("s", lambda: g.scalar.activation(junk[0], in_[0], SIGN, bias=bias[0], scale=-1.0, accum_out=acc[0]),
           [in_, bias], [junk, acc])

    def iota(out, pattern, base, ch=0, whole=False):
        if whole:
            op("g", lambda: g.iota(out[0], pattern, base, ch), [], [out])
        else:
            op("g", lambda: g.iota(out[0], pattern, base, ch, allow_small_or_imprecise_dtypes=True), [], [out])

    def quant_at(name, c0, n, tile, at):
        c, s, t = W(name + "c", c0, c0 + n), W(name + "s", c0, c0 + n), W(tile, at, at + 4 * n)
        op("v", lambda: g.vector.quantize_mx(c[0], s[0], t[0]), [t], [c, s])

    def quant(name, c0, n, tile, e0):
        quant_at(name, c0, n, tile, 4 * e0)

    def mm(bank, a, a0, b, b0, n):
        o = W(bank, 0, n)
        ac, as_, bc, bs = W(a + "c", a0, a0 + 128), W(a + "s", a0, a0 + 128), W(b + "c", b0, b0 + n), W(b + "s", b0, b0 + n)
        op("p", lambda: g.tensor.matmul_mx(o[0], ac[0], as_[0], bc[0], bs[0], True, True), [ac, as_, bc, bs], [o])

    def pickc(dst, c0, src, off, o0, k, wide=None):
        o, w, f = W(dst + "c", c0, c0 + 16 * k), W(src + "c", 0, wide), W(off, o0, o0 + k)
        op("v", lambda: g.vector.tensor_copy(o[0].bitcast(dt.uint32), w[0].bitcast(dt.uint32).indirect(f[0])), [w, f], [o])

    def picks(q, dst, c0, src, off, o0, k, wide=None):
        copy(q, W(dst + "s", c0, c0 + 16 * k), by(W(src + "s", 0, wide), W(off, o0, o0 + k)))

    def pick(dst, c0, src, off, o0, k, wide=None):
        pickc(dst, c0, src, off, o0, k, wide)
        picks("s", dst, c0, src, off, o0, k, wide)

    def weave(*chains):
        chains = [list(c) for c in chains]
        while any(chains):
            for c in chains:
                if c:
                    c.pop(0)()

    ring = [(r + j) % N for j in range(N)]
    seat = (0, 1, 3, 2)
    twice = [ring[seat[k // 2]] for k in range(2 * N)]

    def engines_of(a, b, k, part):
        e = topo.engines(T.cores[a], T.cores[b])
        e = e[0::2] + e[1::2]
        h, f = len(e) // 2, len(e) // 4
        return ((e[:h], e[h:h + f], e[h + f:]), (e[h:], e[:f], e[f:h]))[part][k]

    def send(phase, src, dst, base):
        for part, tag in enumerate("cs"):
            sem = "a%s%d" % (tag, phase)
            moves, reads = [], []
            for j in range(1, N):
                d = ring[j]
                rid, pid, _ = topo.addr(T.cores[d])
                a = W(src + tag, RUN * (j - 1), RUN * j)
                b = W(dst + tag, base + RUN * (N - j - 1), base + RUN * (N - j))
                reads = reads + a[1]
                m = sum(1 << e for e in engines_of(r, d, j - 1, part))
                moves.append(RemoteDMATransfer(
                    dst_ids=[DstId(rid=rid, pnc=pid)], dma_engine_mask=m, remote_sem=T.sem[sem],
                    src=raw(a)[0] if tag == "c" else a[0], dst=raw(b)[0] if tag == "c" else b[0]))
                count["loc"] = count.get("loc", 0) + len(engines_of(r, d, j - 1, part))
            order("g", reads, [])
            g.remote_dma_fused(moves, local_sem=T.sem.loc)
            total = sum(len(engines_of((r - j) % N, r, j - 1, part)) for j in range(1, N))
            count[sem] = total
            note("far", [], W(dst + tag, base, base + FAR)[1], (sem, total, {}))

    PM, PF, IB = W("pm", 0, 1), W("pm", 1, 2), W("pm", 2, 3)
    G = 256
    A = CAP + RUN

    dma("y", W("xt", 0, 512), hbm(T.x[:, 0:512]), "dx0")
    dma("s", W("et", 0, 4 * G), hbm(T.e[:, 0:4 * G]), "del")
    dma("y", W("et", 4 * G, 4 * NS), hbm(T.e[:, 4 * G:4 * NS]), "deh")
    dma("y", W("ph", 0, 24), hbm(T.pa[:, :]), "dp", 2)
    dma("y", W("ph", 24, 48), hbm(T.pb[:, :]), "dp", 2)
    for t in (1, 2):
        dma("y", W("xt", 4 * ST * t, 4 * ST * t + 512), hbm(T.x[:, 512 * t:512 * t + 512]), "dx%d" % t)
    dma("y", W("vt"), hbm(T.v[:, :]), "dv")
    runs = [[0, 1]]
    for k in range(1, 2 * N):
        if twice[k] == twice[k - 1] + 1:
            runs[-1][1] += 1
        else:
            runs.append([k, 1])
    for k, m in runs:
        dma("y", W("pv", 0, 48, 1, 16 * k, 16 * (k + m)), W("ph", 0, 48, 1, 16 * twice[k], 16 * (twice[k] + m)),
            "ddup", len(runs))

    iota(W("pi", 0, 1), [[0, 1]], 0, 1, True)
    iota(W("jid"), [[1, 128]], 0)
    iota(W("j16"), [[0, 8], [1, 16]], 0)
    iota(W("cj0"), [[16, 4]], 0)
    iota(W("ct0"), [[ST - 1, NT], [16, 8]], 0)
    iota(W("c13", 0, 15), [[0, 5], [2 * ST, 3]], 128)
    iota(W("zz"), [[0, 32]], 0)
    iota(W("jj"), [[1, 2 * NS]], -NS)
    for t in range(NT):
        for q in (0, 2):
            iota(W("cx", 8 * t + 2 * q, 8 * t + 2 * q + 4), [[RUN * (seat[q + 1] - seat[q]), 2], [0, 2]],
                 CAP + 16 * t + RUN * seat[q])
    iota(W("val", 0, 16), [[NT, 16]], OLD + 128 - RUN)
    iota(W("val", 16, 64), [[RUN, N - 1], [NT, 16]], OLD + 128)
    iota(W("row1"), [[0, 192]], 0)
    for t in range(NT):
        iota(W("cu", 4 * t, 4 * t + 3), [[RUN, N - 1]], A + 16 * t)
        iota(W("cu", 4 * t + 3, 4 * t + 4), [[0, 1]], CAP + 16 * t)
    iota(W("c1"), [[NS, 4]], 0)
    iota(W("c2"), [[-2 * NS, 2], [NS, 2]], 4 * NS)
    fill(W("ut"), 0.0)
    for t in range(NT):
        fill(W("xt", 4 * (ST * t + 128), 4 * (ST * t + 130)), 0.0)
    copy("v", PF, W("pi", 0, 1))
    ts(W("pi", 1, 2), W("pi", 0, 1), 15, AluOpType.bitwise_and)
    fill(W("zl"), 128)
    for u in range(2):
        ts(W("ut", UW * u + 2 + u, UW * u + 514, 4), W("jid"), PF, EQ, 0.5, MUL)
    copy("v", PM, W("pi", 1, 2))
    for b in range(4):
        quant_at("qu", 128 * b, 128, "ut", UW * (b % 2) + (2 if b < 2 else 0))
    ts(IB, PM, 0.5, ADD)
    act(W("mt"), W("j16"), ACT.Abs, PM, -1.0)
    act(W("rs"), W("j16"), SIGN)
    act(W("cj"), W("cj0"), ACT.Identity, PM)
    act(W("ct"), W("ct0"), ACT.Identity, PM)
    act(W("msk"), W("mt"), ACT.Relu, 1.0, -1.0)

    def steps(lst, w, early, mid, tail):
        def some(which, c0, c1):
            return W(lst, 24 * which + c0 // 16, 24 * which + c1 // 16)

        def first(q, c0, c1):
            copy(q, W(w, c0, c1), by(W("a0"), some(0, c0, c1)))

        def larger(c0, c1):
            tt(W(w, NS + c0, NS + c1), by(W("a0"), some(1, c0, c1)), W(w, c0, c1), MAX)
        first("s", 128, 320)
        first("v", 0, 64)
        first("v", 64, 128)
        first("s", 320, NS)
        early()
        for c0, c1 in ((0, 64), (64, 128), (128, 320), (320, NS)):
            larger(c0, c1)
        for c0, c1 in ((0, 128), (128, 320), (320, NS)):
            tt(W("a1", c0, c1), W(w, NS + c0, NS + c1), W("pf1", c0, c1), ADD)
        copy("s", W("f2"), W("pf2", 0, NS))
        mid()
        for c0, c1 in ((0, 160), (160, 320)):
            copy("s", W(w, 4 * NS + c0, 4 * NS + c1), by(W("a1"), some(0, c0, c1)))
        if tail is None:
            copy("s", W(w, 4 * NS + 320, 5 * NS), by(W("a1"), some(0, 320, NS)))
            copy("s", W(w, 5 * NS, 6 * NS), by(W("a1"), some(1, 0, NS)))
        else:
            tail()
        tt(W("ww"), by(W("a1"), some(1, 0, NS)), W("f2"), ADD)
        tt(W("uu", 320, NS), by(W("a1"), some(0, 320, NS)), W("f2", 320, NS), ADD)
        for c0, c1 in ((0, 160), (160, 320)):
            tt(W("uu", c0, c1), W(w, 4 * NS + c0, 4 * NS + c1), W("pf2", c0, c1), ADD)
        scan(W("rr"), W("uu"), W("ww"), LOW, MAX, MAX)

    def decode(x, stride, src, off, lst, w, mid, idle):
        pickc(x, 0, src, off, 0, 4)
        pickc(x, 64, src, off, 4, 4)
        picks("v", x, 0, src, off, 0, 4)
        picks("s", x, 64, src, off, 4, 4)
        cut = 240
        mm("pa0", x, 0, "qe", 0, cut)
        mm("pb0", x, 0, "qe", cut, NS - cut)
        for t in (1, 2):
            pick(x, stride * t, src, off, 8 * t, 8)
            mm("pf%d" % t, x, stride * t, "qe", 0, NS)
        copy("s", W("a0", 0, cut), W("pa0", 0, cut))
        idle(0)
        copy("v", W("a0", cut, NS), W("pb0", 0, NS - cut))
        idle(1)
        steps(lst, w, lambda: None, mid, None)

    def keep(b):
        copy("s", W("de", NS * b, NS * b + NS), W("pd%d" % b, 0, NS))

    def decode_first():
        def later(t):
            quant("d1", ST * t, 130, "xt", ST * t)
            mm("pf%d" % t, "d1", ST * t, "qe", 0, NS)
            if t == 2:
                for b in range(4):
                    mm("pd%d" % b, "qu", 128 * b, "qe", 0, NS)
        quant("d1", 0, 130, "xt", 0)
        quant("qe", 0, G, "et", 0)
        quant("qe", G, NS - G, "et", G)
        mm("pa0", "d1", 0, "qe", 0, G)
        mm("pb0", "d1", 0, "qe", G, NS - G)
        copy("v", W("lh", 0, 48), W("ph"))
        copy("v", W("a0", 0, G), W("pa0", 0, G))
        copy("s", W("a0", G, NS), W("pb0", 0, NS - G))
        later(1)
        steps("lh", "wh", lambda: later(2), lambda: None, lambda: keep(0))

    def move(name, c0, c1, st, src, dst):
        copy("v", W(name, c0, c1, st, dst, dst + 32), W(name, c0, c1, st, src, src + 32))

    HALVES = ((0, 0, 0), (1, 64, 0), (1, 64, 64), (0, 0, 64))

    def admit(fl, side):
        def gap(k):
            for _ in range(k):
                if side:
                    side.pop(0)()
        gap(1)
        part = NS // N
        for k in range(1, N):
            ts(W("bb", 32 * k - 32, 32 * k), W("zz"), W("rr", part * k - 1, part * k), ADD, W("rr", NS - 1, NS), LT)
        for k in range(N - 1):
            turn_block(W("tr", 32 * k, 32 * k + 32), W("bb", 32 * k, 32 * k + 32))
        for k in (0, 1, 3, 2):
            q = twice.index(k) // 2
            for a in range(N):
                out = W("oh", 32 * a, 32 * a + 32, 1, 32 * q, 32 * q + 32)
                if k > 0:
                    reach = W("tr", 32 * k - 32, 32 * k, 1, 32 * a, 32 * a + 32)
                if k < N - 1:
                    past = W("tr", 32 * k, 32 * k + 32, 1, 32 * a, 32 * a + 32)
                if k == 0:
                    act(out, past, ACT.Identity, 1.0, -1.0)
                elif k == N - 1:
                    copy("s", out, reach)
                else:
                    tt(out, reach, past, SUB)
        gap(1)
        scan(W("cum"), W("oh"), W("oh"), 0.0, ADD, MAX)
        signs(W("one", 1, 2), W("j2"), W("cum"), IB)
        gap(3)
        for k, a, b in HALVES:
            c0, c1 = ((0, 7), (7, 13))[k]
            ts(W(fl, c0, c1, 1, b, b + 64), W("c13", c0 + 2, c1 + 2, 1, a, a + 64), W("one", 1, 2, 1, a, a + 64), ADD,
               0.5, MUL)
        gap(1)
        for a in (0, 64):
            move(fl, 4, 10, 1, a + 32, a)
            move(fl, 10, 13, 1, a, a + 32)
        for a in (0, 64):
            move(fl, 0, 4, 1, a, a + 32)

    def back(w, put, cut):
        one, gg, gs2, gs1, o2, o1 = (c + w for c in ("one", "gg", "gs2", "gs1", "o2", "o1"))
        s2, top = W(one, 2, 3), W("rr", NS - 1, NS)
        low = W(one, 6, 7) if cut else 0.0
        calls = [lambda: signs(s2, W("jk", cut, NS), W("rr", cut, NS), top)]
        if cut:
            calls += [lambda: ts(W("lt", 0, cut), W("rr", 0, cut), top, LT),
                      lambda: op("v", lambda: g.vector.tensor_reduce(low[0], W("lt", 0, cut)[0], AxisListType.X, ADD),
                                 [W("lt", 0, cut)], [low])]
        calls += [
            lambda: ts(W(o2), W("c2"), s2, ADD, low, ADD),
            lambda: tt(W(gg), by(W(w), W(o2)), W("msk", 0, 64), MUL),
            lambda: put(2, s2, low),
            lambda: scan(W(gs2), W("rs", 0, 64), W(gg), 0.0, MUL, ADD),
            lambda: ts(W(one, 5, 6), W(gs2, 31, 32), W(gs2, 15, 16), GT, W(gs2, 63, 64), MUL),
            lambda: ts(W(o1), W("c1"), W(gs2, 47, 48), ADD, W(one, 5, 6), ADD),
            lambda: tt(W(gg), by(W(w), W(o1)), W("msk", 0, 64), MUL),
            lambda: put(1, W(gs2, 47, 48), W(one, 5, 6)),
            lambda: scan(W(gs1), W("rs", 0, 64), W(gg), 0.0, MUL, ADD),
            lambda: ts(W(one, 4, 5), W(gs1, 31, 32), W(gs1, 15, 16), GT, W(gs1, 63, 64), MUL),
            lambda: put(0, W(gs1, 47, 48), W(one, 4, 5))]
        return calls

    def places(fl):
        f = W(fl, 1, 13, 3)
        return [lambda: (ts(W("nf", 4, 8), f, 128.0, EQ), copy("v", W("nf", 0, 4), f)),
                lambda: tt(W("nf", 8, 12), W("nf", 4, 8), W("cj"), MUL),
                lambda: tt(W("nf", 12, 16), W("nf", 8, 12), W("nf", 0, 4), ADD),
                lambda: copy("v", W("so"), W("nf", 12, 16))]

    def merge_list(row, ml):
        win = W(row)
        return ([lambda: op("v", lambda: g.vector.tensor_copy(win[0].indirect(W("so")[0]), W("val")[0]),
                            [W("so"), W("val")], [win])]
                + [lambda c=c: tt(W("mk", c, c + 64), W(row, c, c + 64), W("msk", 0, 64), MUL) for c in (0, 64)]
                + [lambda: scan(W("rho"), W("rs"), W("mk"), 0.0, MUL, ADD)]
                + [lambda t=t: tt(W("mx", 8 * t, 8 * t + 8), W("rho", 15, 128, 16), W("ct", 8 * t, 8 * t + 8), MAX)
                   for t in range(NT)]
                + [lambda t=t: ts(W(ml, 8 * t, 8 * t + 8), W("mx", 8 * t, 8 * t + 8), float(t), ADD) for t in range(NT)])

    def tables(lst, w, src, df):
        return [lambda: tt(W(df), W(src, 24, 48), W(src, 0, 24), SUB),
                lambda: copy("s", W(w, 2 * NS, 3 * NS), by(W("jj", NS, 2 * NS), W(lst, 0, 24))),
                lambda: ts(W(lst, 48, 72), W(df), float(NS), ADD),
                lambda: copy("s", W(w, 3 * NS, 4 * NS), by(W("jj"), W(lst, 48, 72)))]

    def blend(bl, t, mine, bt, fused):
        f = W(bl, 6 * t + 4, 6 * t + 5) if mine else W(bl, 6 * t, 6 * t + 3)
        c0, c1 = (64 * t + RUN, 64 * t + 64) if mine else (64 * t, 64 * t + RUN)
        e0, e1 = (4 * FAR, 4 * (FAR + RUN)) if mine else (0, 4 * FAR)

        def picked(b):
            return by(W("de", NS * b, NS * b + NS), f)

        def part(name, b):
            return W(name, 192 * b + c0, 192 * b + c1)

        def out(b):
            return W(bt, e0 + 4 * t + b, e1, 4 * NT)
        return ([lambda b=b: copy("s", part("ge", b), picked(b)) for b in range(fused, 4)]
                + [lambda b=b: tt(out(b), picked(b), part("dc", b), ADD) for b in range(fused)]
                + [lambda b=b: tt(out(b), part("ge", b), W("pd%d" % b, c0, c1), ADD) for b in range(fused, 4)])

    def product(bank, c0, n):
        mm(bank, "qv", 0, "d2", c0, n)
        copy("s", W("yw", c0, c0 + n), W(bank, 0, n))

    rows = tables("lh", "wh", "ph", "dfh")
    for turn in (1, 2):
        d, s, l, x, n, u = ("%s%d" % (c, turn) for c in "dslxnu")
        fl, bl, bt, ml, row = ("%s%d" % (c, turn) for c in ("fl", "bl", "bt", "ml", "row"))
        home = []
        if turn == 1:
            decode_first()
        else:
            decode("d2", ST, "d1", "ml1", "lh", "wh", lambda: None, lambda k: None)
            home = back("wh", lambda t, a, b: ts(W("po", t, t + 1), W("zz", 0, 1), a, ADD, b, ADD), 0)
        admit(fl, home)
        if turn == 1:
            keep(1)
        pick(s, 0, d, fl, 4, 9, OLD)
        send(2 * turn - 2, s, l, A)
        if turn == 1:
            iota(W("row2"), [[0, 192]], 0)
            iota(W("yw"), [[0, HW]], 0)
        merge = merge_list(row, ml)
        mine = places(fl) + merge[:1]
        if turn == 1:
            there = tables("lv", "wv", "pv", "dfv")
            weave(mine, [lambda: pick(l, 0, d, fl, 0, 4, OLD), lambda: copy("v", W("lv", 0, 48), W("pv")),
                         lambda: ts(W("xl"), W("cx"), PM, ADD), lambda: ts(W("ul"), W("cu"), PM, ADD), rows[2]],
                  there[:1] + rows[:1] + there[1:] + [lambda: quant("qv", 0, 128, "vt", 0)]
                  + [lambda t=t: pick("d2", ST * t + 128, "d1", "zl", 0, 1, OLD) for t in range(NT)])
        else:
            weave(mine, home, [lambda: pick(l, 0, d, fl, 0, 4, OLD)])
            dma("y", hbm(T.ol[:, :]), after(W("po", 0, 3), W("l2s", A, LW)), "out1")
            for t in range(NT):
                product(("pa0", "pb0", "pf1")[t], ST * t, 128)

        def halves():
            picks("s", u, 0, l, "ul", 0, 6)
            picks("s", u, 96, l, "ul", 6, 6)
            for b in range(2 + turn):
                if turn == 1 and b == 2:
                    keep(2)
                mm("pd%d" % b, "qu", 128 * b, u, 0, 192)

        decode(x, 128, l, "xl", "lv", "wv", halves, lambda k: pickc(u, 96 * k, l, "ul", 6 * k, 6))

        sums = ((("gs1wv", 47), ("onewv", 4)), (("gs2wv", 47), ("onewv", 5)), (("onewv", 2), ("onewv", 6)))

        def put(t, some=HALVES):
            (a, i), (b, j) = sums[t]
            for k, p, q in some:
                c0, c1, st = (6 * t + 1, 6 * t + 3, 1) if k else (6 * t, 6 * t + 5, 4)
                ts(W(bl, c0, c1, st, q, q + 64), W("zz", 0, 2, 1, p, p + 64), W(a, i, i + 1, 1, p, p + 64), ADD,
                   W(b, j, j + 1, 1, p, p + 64), ADD)

        def near(t, some):
            for a in some:
                move(bl, 6 * t, 6 * t + 2, 1, a + 32, a)
                move(bl, 6 * t + 2, 6 * t + 5, 2, a, a + 32)

        path = back("wv", None, 64)
        path[0]()
        if turn == 1:
            keep(3)
            mm("pd3", "qu", 384, u, 0, 192)
        for b in range(3):
            copy("s", W("dc", 192 * b, 192 * (b + 1)), W("pd%d" % b, 0, 192))
        new = [blend(bl, t, False, bt, 0 if t else 3) for t in range(NT)]
        fit = {1: merge[1:2], 2: merge[2:3], 3: [lambda: put(2, HALVES[:3])],
               4: [lambda: put(2, HALVES[3:]), lambda: near(2, [0])], 6: [lambda: near(2, [64])] + new[2][:4],
               7: merge[3:4], 8: [lambda: put(1)], 9: [lambda: near(1, [0, 64])] + new[1][:4], 11: new[2][4:7],
               12: new[2][7:] + merge[4:6]}
        for k in (1, 2, 3, 4, 6, 7, 8, 9, 11, 12):
            path[k]()
            weave(fit.get(k, []))
        put(0)
        weave(new[1][4:5])
        near(0, [0, 64])
        weave(new[1][5:] + new[0] + merge[6:7])
        quant(n, 0, FAR, bt, 0)
        send(2 * turn - 1, n, d, OLD + 128)
        weave([c for some in zip(*[blend(bl, t, True, bt, 3) for t in range(NT)]) for c in some] + merge[7:])
        quant(d, OLD, 128, bt, 64)
        if turn == 1:
            weave(rows[1::2])
        else:
            for t, ((a, i), (b, j)) in enumerate(sums):
                ts(W("pd", t, t + 1), W("zz", 0, 1), W(a, i, i + 1), ADD, W(b, j, j + 1), ADD)
            q = 0
            while q < N:
                m = 2 if q + 1 < N and twice[2 * q + 2] == twice[2 * q] + 1 else 1
                dma("y", hbm(T.dl[16 * twice[2 * q]:16 * (twice[2 * q] + m), :]),
                    W("pd", 0, 3, 1, 32 * q + 16, 32 * q + 16 * (m + 1)), "out1")
                q += m

    product("pa0", OLD, 128)
    pickc("d3", 0, "d2", "ml2", 0, 8)
    dma("y", hbm(T.oc[:, 0:512]), raw(W("d3c", 0, 128)), "out1")
    pickc("d3", 128, "d2", "ml2", 8, 6)
    pickc("d3", 224, "d2", "ml2", 14, 10)
    dma("y", hbm(T.oc[:, 512:1536]), raw(W("d3c", 128, 384)), "out1")
    picks("s", "d3", 224, "d2", "ml2", 14, 10)
    product("pb0", OLD + 128, FAR)
    picks("v", "d3", 0, "d2", "ml2", 0, 8)
    picks("s", "d3", 128, "d2", "ml2", 8, 6)
    copy("s", W("ys", 0, 192), by(W("yw"), W("ml2", 0, 12)))
    copy("v", W("ys", 192, 384), by(W("yw"), W("ml2", 12, 24)))
    dma("s", hbm(T.y[:, :]), W("ys"), "out2")
    for k in range(4):
        dma("ys"[k // 3], hbm(T.osc[4 * k:4 * k + 4, :]), W("d3s", 0, None, 1, 32 * k, 32 * k + 4), "out%d" % (1 + k // 3))
    for sem in SEMAPHORES:
        if count.get(sem, 0) > known["g"].get(sem, 0):
            g.wait_ge(T.sem[sem], count[sem])
